import numpy as np, ml_dtypes
CORES = [10,34,74,98]
N = 4
import mx_ref
BF = ml_dtypes.bfloat16
def gentries(a):
    return np.ascontiguousarray(a.reshape(8, 16, -1).transpose(0, 2, 1)).reshape(8, -1)
def gtable(e):
    e = np.asarray(e); return np.ascontiguousarray(e.reshape(8, -1, 16).transpose(0, 2, 1)).reshape(128, -1).astype(np.int32)
def gcols(t, e):
    v = np.concatenate([t.reshape(8, 16, -1, 4), np.zeros((8, 16, 1, 4), BF)], axis=2)
    return np.ascontiguousarray(np.stack([v[g][:, e[g]] for g in range(8)])).reshape(128, -1)
def tile(rs):
    return np.stack(rs, axis=2).reshape(128, -1).astype(BF)
def pick(q, e):
    c = np.concatenate([q[0].reshape(128, -1, 4), np.zeros((128, 1, 4), np.uint8)], axis=1); s = np.concatenate([q[1], np.ones((16, 1), np.uint8)], axis=1)
    return (np.ascontiguousarray(c[:, e].reshape(128, -1)), np.ascontiguousarray(s[:, e]))
def join(*qs):
    return (np.concatenate([q[0] for q in qs], axis=1), np.concatenate([q[1] for q in qs], axis=1))
def put(q, e, v):
    c, s = q[0].reshape(128, -1, 4).copy(), q[1].copy(); c[:, e] = v[0].reshape(128, -1, 4); s[:, e] = v[1]
    return (c.reshape(128, -1), s)
def pk(c, s):
    return (np.ascontiguousarray(c), mx_ref.live(s))
def emit(q):
    return q[0], q[1]
def packed(v, rng):
    q = [mx_ref.quantize(np.ascontiguousarray(v[r])) for r in range(N)]
    return np.stack([a for a, b in q]), np.stack([mx_ref.plane(b, rng) for a, b in q])
def values_of_codes():
    e, c = np.zeros((128, 128, 4), np.float32), np.zeros((128, 2, 4), np.uint8)
    e[np.arange(128), np.arange(128), 0] = 1
    c[:127, :, 0] = np.arange(256).reshape(2, 128).T[:127]
    return mx_ref.matmul(mx_ref.quantize(e.reshape(128, 512).astype(BF)), (c.reshape(128, 8), np.full((16, 2), 127, np.uint8))).T.reshape(-1).astype(np.float64)
CODE_VALUE, SCALE_VALUE = values_of_codes(), 2.0 ** (np.arange(256) - 127.0)
def decode(q):
    return (CODE_VALUE[q[0]].reshape(16, 8, -1, 4) * SCALE_VALUE[q[1]][:, None, :, None] + 0.0).reshape(128, -1).astype(np.float32)
def f(rng, *shape):
    return mx_ref.flush((rng.standard_normal(shape, dtype=np.float32) * np.exp2(rng.integers(-2, 3, shape[:-1] + (1,)))).astype(BF))
def wide(rng, *shape, cols=0):
    v = rng.standard_normal(shape, dtype=np.float32) * np.exp2(rng.integers(-12, 13, shape)).astype(np.float32)
    if cols: v *= np.repeat(np.exp2(rng.integers(-cols, cols + 1, shape[:-2] + (1, shape[-1] // 4))) * (rng.random(shape[:-2] + (1, shape[-1] // 4)) > 0.0625), 4, axis=-1).astype(np.float32)
    return mx_ref.flush(v.astype(BF))
C, HALF, E = 320, 160, 256
MASK = [1, 2, 3]
TIMES = 9
def register(b):
    a = 2 * np.arange(HALF)
    return np.concatenate([a + b, a + 1 - b], axis=-1)
def lowest(s):
    low, to = np.broadcast_to(np.arange(C), s.shape), s
    for i in range(TIMES):
        low = np.minimum(low, np.take_along_axis(low, to, axis=-1))
        to = np.take_along_axis(to, to, axis=-1)
    return low
def joined(s):
    low, c = lowest(s), np.arange(HALF)
    a, b = low[..., :HALF], low[..., HALF:]
    swap = (a != b) & ((a == c) & (c > 0) | (b == c + HALF))
    return np.concatenate([np.where(swap, s[..., HALF:], s[..., :HALF]), np.where(swap, s[..., :HALF], s[..., HALF:])], axis=-1)
def numbers_of(rng):
    return {"x": np.array(f(rng, N, 128, 4 * C)), "u": np.array(f(rng, N, 128, 512)), "v": np.array(f(rng, N, 128, 512))}
def orders(rng):
    return rng.permuted(np.tile(np.arange(C), (N, 8, 1)), axis=2)
def stored(k):
    return {"kl": np.stack([gtable(k[r]) for r in range(N)])}
def layers(rng):
    return np.array(f(rng, N, 128, 2048)).reshape(N, 8, 16, 4, 8, 16, 4)
def weights(rng, w):
    c, p = packed(np.ascontiguousarray(w).reshape(N, 128, 2048), rng)
    return {"wc": c, "ws": p}
def setup_inputs(rng):
    return {**numbers_of(rng), **stored(orders(rng)), **weights(rng, layers(rng))}
def setup_inputs_ties(rng):
    d = numbers_of(rng)
    o = rng.permutation(N)
    k = rng.integers(-1, 2, (N, 8, C)).astype(np.float32)
    k[o[1]] = 1
    x = d["x"].reshape(N, 8, 16, C, 4)
    x[:, :, 0] = 0
    x[:, :, 0, :, 0] = k.astype(BF)
    a = np.exp2(rng.integers(-3, 4, (8, 1)).astype(np.float64))
    j = rng.integers(3, 7, (8, 4, 6))
    j[:, :, 0] = 6
    q = (9 + 2 * rng.integers(0, 4, (8, 4, 6))) * 0.125 * np.exp2(-j.astype(np.float64))
    x[:, :, 8:] = 0
    x[:, :, 8, :, 0] = (-3.0 * a).astype(np.float32).astype(BF)
    x[:, :, 10, :, 0] = (-0.140625 * a).astype(np.float32).astype(BF)
    x[:, :, 10, :, 1] = (-0.125 * a).astype(np.float32).astype(BF)
    c = np.ones(N, np.float32)
    c[o[0]] = 0
    c[o[2]] = -1
    u = d["u"].reshape(N, 128, 128, 4)
    u[:, :, ::16] = 0
    for h in range(0, 128, 16): u[:, h, h, 0] = c.astype(BF)
    w = layers(rng)
    w[:, :, 0] = 0
    w[:, :, :, :, :, 0] = 0
    w[:, :, :, :, :, 8:] = 0
    for g in range(8): w[:, g, 10, 0, g, 8, 0] = -224.0
    for n, i in enumerate((9, 11, 12, 13, 14, 15)):
        x[:, :, i] = (q[:, :, n] * a * -0.0078125)[:, None].astype(np.float32).astype(BF)
        for g in range(8): w[:, g, 10, :, g, i, 1] = (-q[g, :, n]).astype(np.float32).astype(BF)
    return {"x": x.reshape(N, 128, 4 * C), "u": u.reshape(N, 128, 512), "v": d["v"], **stored(orders(rng)), **weights(rng, w)}
def setup_inputs_near(rng):
    d = numbers_of(rng)
    o = rng.permutation(N) % 4
    k = np.where((o == 1) | (o == 2), 1.0, 2.0 ** -30).astype(np.float32)
    x = d["x"].astype(np.float32).reshape(N, 8, 16, C, 4)
    x[:, :, :8] = 0
    s = rng.integers(-1, 2, (N, 8, C)) * k[:, None, None]
    s[o == 3] = 0
    x[:, :, 0, :, 0] = 1.125 * s
    x[:, :, 1, :, 0] = -1.25 * s
    x[:, :, 7, :, 0] = 2.0 ** -30
    w = layers(rng)
    w[:, :, :8] = 0
    w[:, :, :, :, :, :8] = 0
    for r in range(N):
        if o[r] == 3:
            x[r, :, 4, :, 0] = rng.choice([-1.0, 1.0], (8, C)) * 2.0 ** -30
            for g in range(8):
                w[r, g, 4, 0, g, 0, 0] = 1.125 * 2.0 ** -8
                w[r, g, 4, 0, g, 1, 0] = -1.25 * 2.0 ** -8
                w[r, g, 7, 0, g, 6, 0] = 2.0 ** 5
        at = [0, C - 1, int(rng.integers(C)), int(rng.integers(C))]
        for g, j in zip(rng.permutation(8)[:4], at): x[r, g, 0, j, 0] = 2.0 ** 30 * rng.choice([-1.0, 1.0])
    u = d["u"].reshape(N, 128, 128, 4)
    u[:, :, ::16] = 0
    for h in range(0, 128, 16):
        u[:, h, h, 0] = (1.125 * k).astype(np.float32).astype(BF)
        u[:, h + 1, h, 0] = k.astype(BF)
    return {"x": x.reshape(N, 128, 4 * C).astype(BF), "u": u.reshape(N, 128, 512), "v": d["v"], **stored(orders(rng)), **weights(rng, w)}
def setup_inputs_long(rng):
    d = numbers_of(rng)
    k = orders(rng)
    b = rng.integers(0, 2, (N, 8, HALF))
    for c in rng.permutation(HALF):
        low = lowest(register(b))
        b[..., c] ^= (low[..., c] != low[..., c + HALF]).astype(np.int64)
    last = HALF - 1 - (HALF - 1) // 2
    way = [last >> i for i in range(last.bit_length() - 1, -1, -1)]
    for r in range(N):
        t = rng.permutation(8)
        for g in t[2:4]: b[r, g, rng.integers(1, HALF)] ^= 1
        b[r, t[4], 0] ^= 1
        for g in t[5:]: b[r, g] = rng.integers(0, 2, HALF)
        for g in t[5:7]:
            b[r, g, HALF - 1] = 0
            for i, j in zip(way, way[1:]): b[r, g, HALF - 1 - i] = j & 1
            b[r, g, HALF - 1 - last] = 1 - (HALF - 1) % 2
    s = np.zeros((N, 8, C))
    np.put_along_axis(s, k, np.concatenate([b, rng.integers(0, 2, (N, 8, HALF))], axis=2) * 2.0 - 1.0, axis=2)
    x = d["x"].reshape(N, 8, 16, C, 4)
    x[:, :, 0] = 0
    x[:, :, 0, :, 0] = (s * np.exp2(rng.integers(-3, 4, (N, 8, C)).astype(np.float64))).astype(np.float32).astype(BF)
    u = d["u"].reshape(N, 128, 128, 4)
    u[:, :, ::16] = 0
    for h in range(0, 128, 16): u[:, h, h, 0] = 1
    w = layers(rng)
    w[:, :, :, :, :, 0] = (w[:, :, :, :, :, 0].astype(np.float32) * 4).astype(BF)
    return {"x": x.reshape(N, 128, 4 * C), "u": u.reshape(N, 128, 512), "v": d["v"], **stored(k), **weights(rng, w)}
def setup_inputs_ends(rng):
    d = numbers_of(rng)
    o, e = rng.permutation(N) % 4, rng.permutation(N) % 4
    k = orders(rng)
    x = np.zeros((N, 8, 16, C, 4))
    u = d["u"].astype(np.float32).reshape(N, 128, 128, 4)
    v = np.zeros((N, 128, 512))
    w = np.zeros((N, 128, 4, 128, 4), np.float32)
    i = np.arange(128)[np.arange(128) % 16 < 15]
    j = np.arange(14, 128, 16)
    up, down = np.arange(C), np.arange(C)[::-1]
    for r in range(N):
        if e[r] == 0: k[r] = up
        if e[r] == 1: k[r] = down
        if e[r] == 2: k[r] = np.where(rng.permutation(8)[:, None] < 4, up, down)
        h = rng.permutation(8)
        c = np.where(h < 2, 0.0, h % 2 * 2.0 - 1.0)[None, :, None]
        much = (0.9 + 0.1 * rng.random((8, 16, C, 4))) * 2.0 ** 29
        if o[r] == 0: x[r] = -much
        if o[r] == 1: x[r] = much * rng.choice([-1.0, 1.0], (1, 1, C, 1))
        if o[r] == 2: x[r] = -(1.0 + 0.125 * rng.integers(0, 8, (8, 16, C, 4))) * 2.0 ** -30
        if o[r] == 3: x[r] = d["x"][r].astype(np.float32).reshape(8, 16, C, 4)[:, :, :1]
        x[r, :, 15] = 2.0 ** -30
        if o[r] < 2:
            u[r, :, ::16] = c * (0.9 + 0.1 * rng.random((128, 8, 4))) * 2.0 ** 30
            v[r] = (0.9 + 0.1 * rng.random((128, 512))) * 2.0 ** 30
        else:
            v[r] = (1.0 + 0.125 * rng.integers(0, 8, (128, 512))) * 2.0 ** -30
        if o[r] == 2: u[r, :, ::16] = c * (1.0 + 0.125 * rng.integers(0, 8, (128, 8, 4))) * 2.0 ** -30
        if o[r] == 3: u[r, :, ::16] *= np.abs(c).astype(np.float32)
        n = np.array([1.0, 2.0, 4.0])[rng.permutation(8) % 3]
        for b in range(4):
            if o[r] != 2: w[r, i, b, i, b] = -n[i // 16]
            else:
                w[r, i, b, i, b] = -2.0 ** -8
                w[r, j, b, j, b] = 0.0
                w[r, j + 1, b, j, b] = 2.0 ** 8
                w[r, j - 8, b, j - 8, b] = 0.0
                w[r, j + 1, b, j - 8, b] = 2.0 ** 5
    v = v * rng.choice([-1.0, 1.0], (N, 128, 512))
    return {"x": x.astype(np.float32).reshape(N, 128, 4 * C).astype(BF), "u": u.reshape(N, 128, 512).astype(BF), "v": v.astype(np.float32).astype(BF), **stored(k), **weights(rng, w.astype(BF))}
def setup_inputs_spread(rng):
    d = setup_inputs(rng)
    d["x"] = wide(rng, N, 128, 4 * C, cols=6)
    return d
def check_inputs(d):
    b = []
    for k in ("x", "u", "v"):
        a = np.abs(d[k].astype(np.float32))
        if not (np.isfinite(a).all() and ((a == 0) | (a >= 2.0 ** -30) & (a <= 2.0 ** 30)).all()): b.append("a value of " + k)
    none, least, most = [emit(mx_ref.quantize(np.full((128, 16), k, np.float32).astype(BF)))[1][0, 0] for k in (0.0, 2.0 ** -8, 2.0 ** 8)]
    for r in range(N):
        if not (np.sort(gentries(d["kl"][r]), axis=1) == np.arange(C)).all(): b.append("kl: not a permutation")
        if ((d["wc"][r] == 0x7F) | (d["wc"][r] == 0xFF)).any(): b.append("wc: a code that is no number")
        s = mx_ref.live(d["ws"][r])
        if ((s != none) & ((s < least) | (s > most))).any(): b.append("ws: a scale out of range")
    return b
def reference(x, u, v, kl, wc, ws):
    qu = [mx_ref.quantize(u[r]) for r in range(N)]
    lay = [pk(wc[r], ws[r]) for r in range(N)]
    now = [x[r] for r in range(N)]
    k = [gentries(kl[r]).astype(np.int64) for r in range(N)]
    for m in MASK:
        e, made = [], []
        for r in range(N):
            s = mx_ref.matmul(qu[r], mx_ref.quantize(now[r]))[::16]
            bits = (np.take_along_axis(s, k[r][:, :HALF], axis=1) > 0).astype(np.int64)
            e.append(np.take_along_axis(k[r], joined(register(bits)), axis=1))
            z = (gcols(now[r], k[r]).astype(np.float32) + gcols(now[r], e[r]).astype(np.float32)) * np.float32(0.5)
            q = mx_ref.quantize(z.astype(BF))
            made.append(tile([mx_ref.matmul(pick(lay[r], np.arange(128 * b, 128 * b + 128)), q) * np.float32(0.03125) for b in range(4)]))
        k = [np.take_along_axis(k[r ^ m], e[r], axis=1) for r in range(N)]
        for r in range(N):
            far = decode(mx_ref.quantize(np.ascontiguousarray(made[r ^ m][:, :4 * E]))).astype(BF)
            both = np.concatenate([far, made[r][:, 4 * E:]], axis=1)
            now[r] = (now[r].astype(np.float32) + gcols(both, k[r]).astype(np.float32)).astype(BF)
    y, kp = np.zeros((N, 128, C), np.float32), np.zeros((N, 8, C), np.float32)
    oc, osc = np.zeros((N, 128, 4 * C), np.uint8), np.zeros((N, 16, C), np.uint8)
    for r in range(N):
        q = mx_ref.quantize(now[r])
        y[r] = mx_ref.matmul(mx_ref.quantize(v[r]), q)
        kp[r] = k[r]
        oc[r], osc[r] = emit(q)
    return {"y": y, "kp": kp, "oc": oc, "osc": osc}

@@ -1,0 +1,516 @@
+from concourse.mybir import dt, AluOpType, ActivationFunctionType
+
+C, HALF, CROSS = 320, 160, 256
+ROUNDS = 3
+MASKS = [1, 2, 3]
+LONG = [(0, 2), (4, 8), (11, 12), (14, 20)]
+SHORT = [(2, 4), (8, 11), (12, 14)]
+BLOCKS = [b for a, e in LONG + SHORT for b in range(a, e)]
+AT = {b: i for i, b in enumerate(BLOCKS)}
+NB = sum(e - a for a, e in LONG)
+NL, NS = 16 * NB, C - 16 * NB
+RADIX = [3, 3, 3, 3, 3]
+BIG, LESS = 1024.0, 256
+G0 = NL + 16
+F32, BF, I32, U16, F8, U8 = "float32", "bfloat16", "int32", "uint16", "float8_e4m3fn_x4", "uint8"
+
+SCRATCH = {
+    "ub": ("sbuf", [128, 512], BF), "vb": ("sbuf", [128, 512], BF),
+    "uq": ("sbuf", [128, 128], F8), "us": ("sbuf", [128, 128], U8),
+    "vq": ("sbuf", [128, 128], F8), "vs": ("sbuf", [128, 128], U8),
+    "wq": ("sbuf", [128, 512], F8), "wp": ("sbuf", [128, 512], U8),
+    "one": ("sbuf", [128, 512], BF), "eb": ("sbuf", [128, 2048], BF),
+    "eq": ("sbuf", [128, 512], F8), "ep": ("sbuf", [128, 512], U8),
+    "pidx": ("sbuf", [128, 1], I32), "qidx": ("sbuf", [128, 1], I32), "grp": ("sbuf", [128, 1], I32),
+    "yrow": ("sbuf", [128, C], F32), "cwi": ("sbuf", [128, 16], F32), "cst": ("sbuf", [128, 16], F32), "sel": ("sbuf", [128, 12], U16),
+    "rt": ("sbuf", [128, 128], F32), "ru": ("sbuf", [128, 128], F32), "ki": ("sbuf", [128, 5], I32), "kf": ("sbuf", [128, 5], F32),
+    "dr": ("sbuf", [128, HALF], F32), "d1": ("sbuf", [128, HALF], F32), "k1b": ("sbuf", [128, HALF], F32), "k3b": ("sbuf", [128, HALF], F32),
+    "k1": ("sbuf", [128, HALF], BF), "k3": ("sbuf", [128, HALF], F32), "bs0": ("sbuf", [128, NL], BF),
+    "cw": ("sbuf", [128, 16], F32), "ca": ("sbuf", [128, 16], F32), "cb": ("sbuf", [128, 16], F32), "cd": ("sbuf", [128, 16], F32),
+    "c2": ("sbuf", [128, 16], F32), "ct0": ("sbuf", [128, 16], F32), "ct1": ("sbuf", [128, 16], F32),
+    "dl": ("sbuf", [128, 64], F32), "dat": ("sbuf", [128, 64], F32), "sc": ("sbuf", [128, 64], F32),
+    "fi": ("sbuf", [128, 16], I32), "fa": ("sbuf", [128, 16], I32),
+    "kli": ("sbuf", [128, 20], I32), "klb": ("sbuf", [128, 32], BF), "klt": ("sbuf", [128, 32], BF),
+    "w0": ("sbuf", [128, G0 + C + 16], BF), "gg": ("sbuf", [128, 5 * 352], BF), "krs": ("sbuf", [128, 3 * C], BF),
+    "bits": ("sbuf", [128, C], BF), "bs1": ("sbuf", [128, NL], BF), "bs2": ("sbuf", [128, NL], BF),
+    "tt": ("sbuf", [128, 864], BF), "of0": ("sbuf", [128, 16], U16), "of1": ("sbuf", [128, 16], U16), "ofs": ("sbuf", [128, 16], U16),
+    "kpf": ("sbuf", [128, C], F32), "yo": ("sbuf", [128, C], F32),
+    "ps": ("psum", [128, 4096], F32),
+}
+for _r in range(ROUNDS + 1):
+    SCRATCH["xt%d" % _r] = ("sbuf", [128, 4 * C], BF)
+    SCRATCH["xq%d" % _r] = ("sbuf", [128, C], F8)
+    SCRATCH["xs%d" % _r] = ("sbuf", [128, C], U8)
+    SCRATCH["kof%d" % _r] = ("sbuf", [128, 32], U16)
+for _r in range(ROUNDS):
+    SCRATCH["k4%d" % _r] = ("sbuf", [128, 128], U16)
+    SCRATCH["tof%d" % _r] = ("sbuf", [128, 20], U16)
+    SCRATCH["kk%d" % _r] = ("sbuf", [128, C], BF)
+    SCRATCH["yp%d" % _r] = ("sbuf", [128, 4 * C], BF)
+    SCRATCH["yi%d" % _r] = ("sbuf", [128, 4 * C], BF)
+    SCRATCH["zt%d" % _r] = ("sbuf", [128, 4 * C], BF)
+    SCRATCH["zq%d" % _r] = ("sbuf", [128, 384], F8)
+    SCRATCH["zs%d" % _r] = ("sbuf", [128, 384], U8)
+    SCRATCH["ht%d" % _r] = ("sbuf", [128, 4 * CROSS], BF)
+    SCRATCH["hq%d" % _r] = ("sbuf", [128, CROSS], F8)
+    SCRATCH["hs%d" % _r] = ("sbuf", [128, CROSS], U8)
+    SCRATCH["rq%d" % _r] = ("sbuf", [128, CROSS], F8)
+    SCRATCH["rs%d" % _r] = ("sbuf", [128, CROSS], U8)
+    SCRATCH["bp%d" % _r] = ("sbuf", [128, 4 * C], BF)
+    SCRATCH["lk%d" % _r] = ("dram", [128, 20], BF)
+    SCRATCH["rk%d" % _r] = ("dram", [128, 20], BF)
+SEMAPHORES = ["sv", "sa", "sp", "sg", "sent", "lx0", "lx1", "lu", "lv", "lk", "lwc", "lws",
+              "oc0", "oc1", "os", "oy0", "oy1", "okp"]
+for _r in range(ROUNDS):
+    SEMAPHORES += ["dk%d" % _r, "dr%d" % _r, "arl%d" % _r, "ar0%d" % _r, "ar1%d" % _r]
+
+
+def rank_program(g, core, T, topo):
+    rank = T.rank_of(core)
+    if rank is None:
+        return
+    A, ACT = AluOpType, ActivationFunctionType
+    queue = {"v": g.vector, "a": g.scalar, "p": g.tensor, "g": g, "s": g.sync}
+    own = {"v": "sv", "a": "sa", "p": "sp", "g": "sg"}
+    total, seen, hist = {}, {q: {} for q in queue}, {}
+
+    def need(q, reads, writes, compute):
+        deps = {}
+        for (names, isw) in ((reads, False), (writes, True)):
+            for (b, lo, hi) in names:
+                for (l, h, w, eq, sem, val) in hist.get(b, []):
+                    if l < hi and lo < h and (w or isw):
+                        if compute and eq == q and isw:
+                            continue
+                        deps[sem] = max(deps.get(sem, 0), val)
+        for sem in deps:
+            if seen[q].get(sem, 0) < deps[sem]:
+                queue[q].wait_ge(T.sem[sem], deps[sem])
+                seen[q][sem] = deps[sem]
+
+    def note(q, reads, writes, sem, val):
+        for (b, lo, hi) in writes:
+            hist[b] = [e for e in hist.get(b, []) if not (lo <= e[0] and e[1] <= hi and (e[3] != q or e[2] is False or (lo, hi) == (e[0], e[1])))]
+            hist[b].append((lo, hi, True, q, sem, val))
+        for (b, lo, hi) in reads:
+            keep = [e for e in hist.get(b, []) if not (not e[2] and e[3] == q and lo <= e[0] and e[1] <= hi)]
+            keep.append((lo, hi, False, q, sem, val))
+            hist[b] = keep
+
+    def op(q, call, reads, writes):
+        need(q, reads, writes, True)
+        sem = own[q]
+        total[sem] = total.get(sem, 0) + 1
+        call(queue[q]).then_inc(T.sem[sem], 1)
+        note(q, reads, writes, sem, total[sem])
+
+    def dma(q, sem, pairs):
+        for (out, in_, reads, writes) in pairs:
+            need(q, reads, writes, False)
+        for (out, in_, reads, writes) in pairs:
+            total[sem] = total.get(sem, 0) + 16
+            queue[q].dma_start(out, in_).then_inc(T.sem[sem], 16)
+        for (out, in_, reads, writes) in pairs:
+            note("d" + q, reads, writes, sem, total[sem])
+
+    def send(dst, out, in_, reads, sem):
+        need("g", reads, [], False)
+        rid, pid = topo.addr(dst)[0], topo.addr(dst)[1]
+        n = len(topo.engines(core, dst))
+        g.remote_dma(out, in_, T.sem[sem], T.sem.sent, pid, rid, topo.mask(core, dst))
+        total["sent"] = total.get("sent", 0) + n
+        total[sem] = total.get(sem, 0) + n
+
+    def tts(out, in0, s1, s2, o0, o1, reads, writes):
+        if o1 is None:
+            op("v", lambda e: e.tensor_scalar(out, in0, s1, None, o0), reads, writes)
+        else:
+            op("v", lambda e: e.tensor_scalar(out, in0, s1, s2, o0, o1), reads, writes)
+
+    def ttt(out, in0, in1, o, reads, writes):
+        op("v", lambda e: e.tensor_tensor(out, in0, in1, o), reads, writes)
+
+    def act(out, in_, f, reads, writes, **k):
+        op("a", lambda e: e.activation(out, in_, f, **k), reads, writes)
+
+    def quant(q, s, a, b, t, ta, tb):
+        op("v", lambda e: e.quantize_mx(T[q][:, a:b], T[s][:, a:b], T[t][:, ta:tb]), [(t, ta, tb)], [(q, a, b), (s, a, b)])
+
+    def bank(i):
+        return ("ps", 512 * i, 512 * i + 512)
+
+    def mul(i, n, lq, ls, l, rq, rs, a, b):
+        op("p", lambda e: e.matmul_mx(T.ps[:, 512 * i:512 * i + n], T[lq][:, l:l + 128], T[ls][:, l:l + 128],
+                                      T[rq][:, a:b], T[rs][:, a:b], True, True),
+           [(lq, l, l + 128), (ls, l, l + 128), (rq, a, b), (rs, a, b)], [bank(i)])
+
+    peer = [T.cores[rank ^ m] for m in MASKS]
+    dma("s", "lx0", [(T.xt0[:, 0:768], T.x[:, 0:768], [], [("xt0", 0, 768)])])
+    dma("a", "lk", [(T.kli[:], T.kl[:, :], [], [("kli", 0, 20)])])
+    dma("s", "lx1", [(T.xt0[:, 768:1280], T.x[:, 768:1280], [], [("xt0", 768, 1280)])])
+    dma("a", "lu", [(T.ub[:], T.u[:, :], [], [("ub", 0, 512)])])
+    dma("s", "lwc", [(T.wq[:, 0:512].bitcast(dt.uint8), T.wc[:, 0:2048], [], [("wq", 0, 512)])])
+    dma("s", "lws", [(T.wp[:, 0:512], T.ws[:, 0:512], [], [("wp", 0, 512)])])
+    dma("a", "lv", [(T.vb[:], T.v[:, :], [], [("vb", 0, 512)])])
+
+    later = []
+
+    def drip(n):
+        for call in later[:n]:
+            call()
+        later[:n] = []
+
+    def col(i):
+        return T.cst[:, i:i + 1]
+
+    def cc(*i):
+        return [("cst", j, j + 1) for j in i]
+
+    def scol(i, in0, names, s1, s2, o0, o1):
+        tts(col(i), in0, s1, s2, o0, o1, names, cc(i))
+    P1, Q1, GR, YR = ("pidx", 0, 1), ("qidx", 0, 1), ("grp", 0, 1), ("yrow", 0, C)
+    op("g", lambda e: e.iota(T.pidx[:], [[0, 1]], 0, 1), [], [P1])
+    op("g", lambda e: e.iota(T.yrow[:], [[1, C]], 0, 0, allow_small_or_imprecise_dtypes=True), [], [YR])
+    op("g", lambda e: e.iota(T.cwi[:], [[16, 16]], 0, 1, allow_small_or_imprecise_dtypes=True), [], [("cwi", 0, 16)])
+    op("v", lambda e: e.memset(T.rt[:], 0.0), [], [("rt", 0, 128)])
+    op("v", lambda e: e.memset(T.one[:], 1.0), [], [("one", 0, 512)])
+    op("v", lambda e: e.memset(T.klb[:], 0.0), [], [("klb", 0, 32)])
+    cuts = sorted([(a, e, 16 * (AT[a] - a)) for a, e in LONG] + [(a, e, G0) for a, e in SHORT])
+    for a, e, d in cuts:
+        op("v", lambda x: x.memset(T.dr[:, 8 * a:8 * e], float(d)), [], [("dr", 8 * a, 8 * e)])
+    tts(T.qidx[:], T.pidx[:], 15, None, A.bitwise_and, None, [P1], [Q1])
+    tts(T.grp[:], T.pidx[:], 4, None, A.arith_shift_right, None, [P1], [GR])
+    scol(0, T.qidx[:], [Q1], 0.0, None, A.is_equal, None)
+    scol(1, T.qidx[:], [Q1], 0.0, BIG, A.is_equal, A.mult)
+    scol(8, T.grp[:], [GR], 1.0, None, A.mult, None)
+    scol(9, T.grp[:], [GR], 16.0, None, A.mult, None)
+    scol(2, col(0), cc(0), 1.0, None, A.add, None)
+    scol(3, col(0), cc(0), float(-LESS), None, A.mult, None)
+    scol(4, col(0), cc(0), 2.0, 2.0, A.mult, A.add)
+    scol(5, col(0), cc(0), float(1 - 2 * LESS - HALF), float(HALF), A.mult, A.add)
+    scol(6, col(0), cc(0), -LESS - BIG, BIG, A.mult, A.add)
+
+    def widen(nm, a, b, src, c, scale, bias, names):
+        act(T[nm][:, a:b], T[src][:, c:c + b - a], ACT.Identity, [(src, c, c + b - a)] + names, [(nm, a, b)], bias=bias, scale=scale)
+
+    def blank(nm, a, b):
+        act(T[nm][:, a:b], T.yrow[:, 0:b - a], ACT.Copy, [YR], [(nm, a, b)], scale=0.0)
+    lists = [LONG, SHORT]
+    for h in (0, 10):
+        runs = []
+        for b in range(h, h + 10):
+            if runs and AT[b] == runs[-1][1]:
+                runs[-1][1] += 1
+            else:
+                runs.append([AT[b], AT[b] + 1])
+        lists.append(runs)
+
+    def row_of(i):
+        for j in (32 * i, 32 * i + 16):
+            for a, e in lists[i]:
+                w = ("rt", j, j + e - a)
+                if i < 2:
+                    act(T.rt[:, j:j + e - a], T.yrow[:, a:e], ACT.Copy, [YR, w], [w])
+                else:
+                    op("g", lambda x: x.iota(T.rt[:, j:j + e - a], [[1, e - a]], a, 0, allow_small_or_imprecise_dtypes=True), [w], [w])
+                j += e - a
+    row_of(2)
+    row_of(3)
+    widen("k1b", 0, HALF, "yrow", 0, col(2), col(3), cc(2, 3))
+    widen("d1", 0, HALF, "dr", 0, col(0), 0.0, cc(0))
+    widen("k3b", 0, HALF, "yrow", 0, col(4), col(5), cc(4, 5))
+    row_of(0)
+    row_of(1)
+    blank("tt", 672, 864)
+    ttt(T.k1[:], T.k1b[:], T.d1[:], A.add, [("k1b", 0, HALF), ("d1", 0, HALF)], [("k1", 0, HALF)])
+    tts(T.d1[:], T.d1[:], 2.0, None, A.mult, None, [("d1", 0, HALF)], [("d1", 0, HALF)])
+    KL = [("kli", 0, 20)]
+    tts(T.klb[:, 0:20], T.kli[:], -160.0, None, A.add, None, KL, [("klb", 0, 20)])
+    tts(T.kof0[:, 0:20], T.kli[:], 0.0, None, A.add, None, KL, [("kof0", 0, 20)])
+    ttt(T.k3[:], T.k3b[:], T.d1[:], A.add, [("k3b", 0, HALF), ("d1", 0, HALF)], [("k3", 0, HALF)])
+    op("v", lambda e: e.transpose(T.klt[:], T.klb[:]), [("klb", 0, 32)], [("klt", 0, 32)])
+    WIDE = 32 * ((NB + 1) // 2)
+    RU, KI, KF = [("ru", 0, 128)], [("ki", 0, 4)], [("kf", 0, 4)]
+    KQ = [("ki", 4, 5), ("kf", 4, 5)]
+
+    def seln(o, in0, s1, s2, o0, o1, names):
+        tts(o, in0, s1, s2, o0, o1, names, [("sel", 0, 12)])
+    tts(T.ki[:, 4:5], T.qidx[:], col(8), None, A.add, None, [Q1] + cc(8), [("ki", 4, 5)])
+    tts(T.kf[:, 4:5], T.qidx[:], 16.0, None, A.mult, None, [Q1], [("kf", 4, 5)])
+
+    def own_places():
+        tts(T.ki[:, 4:5], T.ki[:, 4:5], 1, None, A.bitwise_and, None, [("ki", 4, 5)], [("ki", 4, 5)])
+        for t in range(4):
+            tts(T.k40[:, 32 * t:32 * t + 20], T.kli[:], 4.0, float(t), A.mult, A.add, KL, [("k40", 32 * t, 32 * t + 20)])
+        seln(T.sel[:, 6:7], T.ki[:, 4:5], float(WIDE + 16), T.kf[:, 4:5], A.mult, A.add, KQ)
+        seln(T.sel[:, 0:1], T.ki[:, 4:5], float(C + 16), T.kf[:, 4:5], A.mult, A.add, KQ)
+
+    where = [
+        lambda: op("v", lambda e: e.transpose(T.ru[:], T.rt[:]), [("rt", 0, 128)], RU),
+        lambda: (tts(T.ki[:, 0:4], T.ru[:, 0:128:32], col(8), None, A.add, None, RU + cc(8), KI),
+                 tts(T.kf[:, 0:4], T.ru[:, 0:128:32], 16.0, None, A.mult, None, RU, KF)),
+        lambda: tts(T.ki[:, 0:4], T.ki[:, 0:4], 1, None, A.bitwise_and, None, KI, KI),
+        lambda: tts(T.ki[:, 0:4], T.ki[:, 0:4], C + 16, None, A.mult, None, KI, KI),
+        lambda: ttt(T.kf[:, 0:4], T.kf[:, 0:4], T.ki[:, 0:4], A.add, KI + KF, KF),
+        lambda: seln(T.sel[:, 2:6:2], T.kf[:, 0:2], 0.0, None, A.add, None, KF)]
+
+    def find(i):
+        where[i]()
+    later += [lambda: seln(T.sel[:, 8:12:2], T.kf[:, 2:4], 1.0, None, A.add, None, KF),
+              lambda: seln(T.sel[:, 1:2], T.sel[:, 0:1], 256.0, None, A.add, None, [("sel", 0, 12)])]
+    SE = ("sel", 0, 12)
+    for a, e in LONG:
+        widen("bs0", 16 * AT[a], 16 * (AT[a] + e - a), "yrow", 16 * a, 1.0, col(1), cc(1))
+    widen("w0", 0, NL, "yrow", 0, col(0), col(6), cc(0, 6))
+    blank("w0", NL, G0)
+    blank("w0", G0 + C, G0 + C + 16)
+    for i in range(2):
+        blank("gg", 352 * i, 352 * i + 16)
+        blank("gg", 352 * i + 16 + NL, 352 * i + 352)
+    CW = [("cw", 0, 16)]
+    later += [
+        lambda: tts(T.cw[:], T.cwi[:], col(9), None, A.subtract, None, [("cwi", 0, 16)] + cc(9), CW),
+        lambda: op("v", lambda e: e.memset(T.dl[:, 0:64:4], 0.0), [], [("dl", 0, 64)]),
+        lambda: tts(T.c2[:], T.cw[:], 2.0, -160.0, A.mult, A.add, CW, [("c2", 0, 16)]),
+        lambda: op("v", lambda e: e.memset(T.dl[:, 3:64:4], -1.0), [], [("dl", 0, 64)]),
+        lambda: tts(T.dat[:, 3:64:4], T.cw[:], 4.0, -319.0, A.mult, A.add, CW, [("dat", 0, 64)]),
+        lambda: tts(T.ca[:], T.cw[:], 0.0, None, A.is_equal, None, CW, [("ca", 0, 16)]),
+        lambda: tts(T.dl[:, 1:64:4], T.cw[:], 159.0, 2.0, A.is_equal, A.mult, CW, [("dl", 0, 64)]),
+        lambda: tts(T.cb[:], T.cw[:], 159.0, -160.0, A.is_equal, A.mult, CW, [("cb", 0, 16)]),
+        lambda: ttt(T.ca[:], T.cw[:], T.ca[:], A.subtract, CW + [("ca", 0, 16)], [("ca", 0, 16)]),
+        lambda: tts(T.dl[:, 1:64:4], T.dl[:, 1:64:4], -1.0, None, A.add, None, [("dl", 0, 64)], [("dl", 0, 64)]),
+        lambda: tts(T.cd[:], T.cw[:], 159.0, 161.0, A.is_equal, A.mult, CW, [("cd", 0, 16)]),
+        lambda: ttt(T.ct0[:], T.ca[:], T.cb[:], A.add, [("ca", 0, 16), ("cb", 0, 16)], [("ct0", 0, 16)]),
+        lambda: ttt(T.ct1[:], T.ca[:], T.cd[:], A.add, [("ca", 0, 16), ("cd", 0, 16)], [("ct1", 0, 16)])]
+
+    dma("s", "dk0", [(T.lk0[16 * i:16 * i + 16, :], T.klt[32 * (i // 2):32 * (i // 2) + 20, 16 * (i % 2):16 * (i % 2) + 16],
+                      [("klt", 0, 32)], [("lk0", 20 * i, 20 * i + 20)]) for i in range(8)])
+
+    def share(r):
+        send(peer[r], T["rk%d" % r][:, :], T["lk%d" % r][:, :], [("lk%d" % r, 0, 160)], "arl%d" % r)
+        note("net", [], [("rk%d" % r, 0, 160)], "arl%d" % r, total["arl%d" % r])
+
+    def fetch(r):
+        dma("s", "dr%d" % r, [(T.krs[0:128:16, C * r:C * r + C], T["rk%d" % r][:, :],
+                               [("rk%d" % r, 0, 160)], [("krs", C * r, C * r + C)])])
+
+    share(0)
+    for b in range(4):
+        op("g", lambda e: e.affine_select(T.eb[:, 512 * b:512 * b + 512], T.one[:], [[1, 512]], A.is_equal, 0.0, -b, -4),
+           [("one", 0, 512)], [("eb", 512 * b, 512 * b + 512)])
+
+    def flip(to, nm, c, n):
+        op("v", lambda e: e.transpose(T.tt[:, to:to + n], T[nm][:, c:c + n]), [(nm, c, c + n)], [("tt", to, to + n)])
+
+    def turn(nm, c0, cut, ahead=None, between=None):
+        if ahead is not None:
+            ahead()
+        flip(0, nm, c0 + 16, cut)
+        flip(C, nm, c0, cut)
+        if between is not None:
+            between()
+        flip(cut, nm, c0 + 16 + cut, C - cut)
+        flip(C + cut, nm, c0 + cut, C + 32 - cut)
+
+    TT, TN = T.tt[:, 0:864], ("tt", 0, 864)
+
+    def wrapped(nm, a, wide, sel, by, plus):
+        tts(T[nm][:, a:a + 16 * wide], TT.indirect(T.sel[:, sel:sel + wide]), by, plus, A.mult, A.add,
+            [TN, SE], [(nm, a, a + 16 * wide)])
+
+    PARTS = [(0, 192), (192, C)]
+
+    def qstate(r, i):
+        a, b = PARTS[i]
+        quant("xq%d" % r, "xs%d" % r, a, b, "xt%d" % r, 4 * a, 4 * b)
+
+    def score(r, i):
+        a, b = PARTS[i]
+        mul(4 + i, b - a, "uq", "us", 0, "xq%d" % r, "xs%d" % r, a, b)
+
+    def sign(i):
+        a, b = PARTS[i]
+        tts(T.bits[:, a:b], T.ps[:, 512 * (4 + i):512 * (4 + i) + b - a], 0.0, col(0), A.is_gt, A.mult, [bank(4 + i)] + cc(0), [("bits", a, b)])
+
+    quant("uq", "us", 0, 128, "ub", 0, 512)
+    for i in range(2):
+        qstate(0, i)
+        score(0, i)
+    own_places()
+    for i in range(2):
+        find(i)
+        sign(i)
+
+    def register(r):
+        kof = "kof%d" % r
+        H1 = G0 + HALF
+        ttt(T.w0[:, G0:H1], T.bits[:, 0:C].indirect(T[kof][:, 0:10]), T.k1[:], A.add,
+            [("bits", 0, C), (kof, 0, 10), ("k1", 0, HALF)], [("w0", G0, H1)])
+
+        def half(t):
+            act(T["yp%d" % r][:, C * t:C * t + C], T["xt%d" % r][:, 0:4 * C].indirect(T["k4%d" % r][:, 32 * t:32 * t + 20]), ACT.Copy,
+                [("xt%d" % r, 0, 4 * C), ("k4%d" % r, 32 * t, 32 * t + 20)], [("yp%d" % r, C * t, C * t + C)], scale=0.5)
+
+        def again(t):
+            act(T["yi%d" % r][:, C * t:C * t + C], T["yp%d" % r][:, C * t:C * t + C], ACT.Copy,
+                [("yp%d" % r, C * t, C * t + C)], [("yi%d" % r, C * t, C * t + C)])
+
+        def blanks(i):
+            if r == 0:
+                blank("gg", 352 * i + 704, 352 * i + 720)
+                blank("gg", 352 * i + 1040, 352 * i + 1056)
+                blank("krs", C * i, C * i + C)
+        half(0)
+        half(1)
+        aside = [lambda: half(2), lambda: (half(3), again(0)), lambda: (again(1), again(2), blanks(0)),
+                 lambda: (again(3), blanks(1)), lambda: blanks(2)]
+        gap = find if r == 0 else (lambda i: None)
+        gap(2)
+        ttt(T.w0[:, H1:G0 + C], T.k3[:], T.w0[:, G0:H1], A.subtract, [("k3", 0, HALF), ("w0", G0, H1)], [("w0", H1, G0 + C)])
+        gap(3)
+        turn("w0", G0 - 16, HALF, None, lambda: gap(4))
+        gap(5)
+        wrapped("of0", 0, 1, 2, 1.0, float(LESS))
+        wrapped("ofs", 0, 1, 4, 1.0, float(LESS))
+        op("v", lambda e: e.tensor_copy(T.fi[:], TT.indirect(T.sel[:, 0:1])), [TN, SE], [("fi", 0, 16)])
+        cur, nxt = 352, 0
+        ttt(T.gg[:, 16:16 + NL], T.w0[:, 0:G0 + C].indirect(T.of0[:, 0:NB]), T.bs0[:], A.min,
+            [("w0", 0, G0 + C), ("of0", 0, 16), ("bs0", 0, NL)], [("gg", 16, 16 + NL)])
+        cur, nxt = nxt, cur
+        tts(T.fa[:], T.fi[:], 1, None, A.bitwise_and, None, [("fi", 0, 16)], [("fa", 0, 16)])
+        for i, rad in enumerate(RADIX):
+            base, of = "bs%d" % (1 + i % 2), "of%d" % ((i + 1) % 2)
+            act(T[base][:], T.gg[:, cur + 16:cur + 16 + NL], ACT.Identity, [("gg", cur + 16, cur + 16 + NL)] + cc(1), [(base, 0, NL)], bias=col(1))
+            aside[i]()
+            flip(0, "gg", cur + 16, WIDE)
+            flip(WIDE, "gg", cur, WIDE)
+            if i == 0:
+                tts(T.dl[:, 2:64:4], T.fa[:], -2.0, 1.0, A.mult, A.add, [("fa", 0, 16)], [("dl", 0, 64)])
+            drip(1)
+            wrapped(of, 0, 1, 6, 1.0, float(LESS))
+            for j in range(rad - 1):
+                if i == 2 and j == 0:
+                    ttt(T.dat[:, 2:64:4], T.fa[:], T.c2[:], A.add, [("fa", 0, 16), ("c2", 0, 16)], [("dat", 0, 64)])
+                else:
+                    drip(1)
+                ttt(T.gg[:, nxt + 16:nxt + 16 + NL], T.gg[:, cur + 16:cur + 16 + NL].indirect(T[of][:, 0:NB]), T[base][:], A.min,
+                    [("gg", cur + 16, cur + 16 + NL), (of, 0, 16), (base, 0, NL)], [("gg", nxt + 16, nxt + 16 + NL)])
+                cur, nxt = nxt, cur
+        turn("gg", cur, 192, lambda: op("v", lambda e: e.tensor_copy(T.gg[:, cur + 16 + NL:cur + 336], T.gg[:, cur + 16:cur + 16 + NL].indirect(T.ofs[:, 0:NS // 16])),
+                                        [("gg", cur + 16, cur + 16 + NL), ("ofs", 0, 16)], [("gg", cur + 16 + NL, cur + 336)]))
+        drip(len(later))
+        for c, ct, sl in ((10, "ct1", 0), (8, "ct0", 1)):
+            ttt(T.dat[:, sl:64:4], TT.indirect(T.sel[:, c:c + 1]), T[ct][:], A.is_equal, [TN, SE, (ct, 0, 16)], [("dat", 0, 64)])
+        op("v", lambda e: e.tensor_tensor_scan(T.sc[:], T.dl[:], T.dat[:], 0.0, A.mult, A.add), [("dl", 0, 64), ("dat", 0, 64)], [("sc", 0, 64)])
+        tof = "tof%d" % r
+        for h in range(2):
+            tts(T[tof][:, 10 * h:10 * h + 10], T.sc[:, 2 + h:39 + h:4], 160.0, None, A.add, None, [("sc", 0, 64)], [(tof, 10 * h, 10 * h + 10)])
+
+    def pairs(r, a, b, some):
+        for t in some:
+            yp, yi, tof = "yp%d" % r, "yi%d" % r, "tof%d" % r
+            ttt(T["zt%d" % r][:, 4 * a + t:4 * b:4], T[yp][:, C * t:C * t + C].indirect(T[tof][:, a // 16:b // 16]),
+                T[yi][:, C * t + a:C * t + b], A.add, [(yp, C * t, C * t + C), (yi, C * t + a, C * t + b), (tof, a // 16, b // 16)], [("zt%d" % r, 4 * a, 4 * b)])
+
+    def layer(r, zcol, bk):
+        for b in range(4):
+            mul(bk + b, 128, "wq", "wp", 128 * b, "zq%d" % r, "zs%d" % r, zcol, zcol + 128)
+
+    def keep(r, a, bk):
+        for b in range(4):
+            act(T["ht%d" % r][:, 4 * a + b:4 * a + 512:4], T.ps[:, 512 * (bk + b):512 * (bk + b) + 128], ACT.Copy,
+                [bank(bk + b)], [("ht%d" % r, 4 * a, 4 * a + 512)], scale=0.03125)
+
+    def ship(r, i):
+        a = 128 * i
+        quant("hq%d" % r, "hs%d" % r, a, a + 128, "ht%d" % r, 4 * a, 4 * a + 512)
+        sem = "ar%d%d" % (i, r)
+        send(peer[r], T["rq%d" % r][:, a:a + 128].bitcast(dt.uint8), T["hq%d" % r][:, a:a + 128].bitcast(dt.uint8), [("hq%d" % r, a, a + 128)], sem)
+        send(peer[r], T["rs%d" % r][:, a:a + 128], T["hs%d" % r][:, a:a + 128], [("hs%d" % r, a, a + 128)], sem)
+
+    def unpack(r, i, bk):
+        a = 128 * i
+        sem = "ar%d%d" % (i, r)
+        note("net", [], [("rq%d" % r, a, a + 128), ("rs%d" % r, a, a + 128)], sem, total[sem])
+        for b in range(4):
+            mul(bk + b, 128, "eq", "ep", 128 * b, "rq%d" % r, "rs%d" % r, a, a + 128)
+        for b in range(4):
+            act(T["bp%d" % r][:, C * b + a:C * b + a + 128], T.ps[:, 512 * (bk + b):512 * (bk + b) + 128], ACT.Copy,
+                [bank(bk + b)], [("bp%d" % r, C * b + a, C * b + a + 128)])
+
+    def advance(r, i, some):
+        a, b = PARTS[i]
+        for t in some:
+            bp, kof = "bp%d" % r, "kof%d" % (r + 1)
+            ttt(T["xt%d" % (r + 1)][:, 4 * a + t:4 * b:4], T[bp][:, C * t:C * t + C].indirect(T[kof][:, a // 16:b // 16]),
+                T["xt%d" % r][:, 4 * a + t:4 * b:4], A.add,
+                [(bp, C * t, C * t + C), (kof, a // 16, b // 16), ("xt%d" % r, 4 * a, 4 * b)], [("xt%d" % (r + 1), 4 * a, 4 * b)])
+
+    for r in range(ROUNDS):
+        register(r)
+        if r == 0:
+            fetch(0)
+        nr = 352 * (2 + r)
+        kr, kk, kof, tof = C * r, "kk%d" % r, "kof%d" % r, "tof%d" % r
+        act(T[kk][:], T.krs[:, kr:kr + C].indirect(T[kof][:, 0:20]), ACT.Copy, [("krs", kr, kr + C), (kof, 0, 20)], [(kk, 0, C)])
+        act(T.gg[:, nr + 16:nr + 336], T[kk][:, 0:C].indirect(T[tof][:, 0:20]), ACT.Copy, [(kk, 0, C), (tof, 0, 20)], [("gg", nr + 16, nr + 336)])
+        zq, zs, zt = "zq%d" % r, "zs%d" % r, "zt%d" % r
+        pairs(r, 0, 128, range(4))
+        for i in range(2):
+            nxt = (128, 256) if i == 0 else (CROSS, C)
+            pairs(r, nxt[0], nxt[1], [0])
+            quant(zq, zs, 128 * i, 128 * i + 128, zt, 512 * i, 512 * i + 512)
+            layer(r, 128 * i, 4 * i)
+            keep(r, 128 * i, 4 * i)
+            pairs(r, nxt[0], nxt[1], [1, 2, 3] if i == 0 else [1, 2])
+        ship(r, 0)
+        pairs(r, CROSS, C, [3])
+        ship(r, 1)
+        quant(zq, zs, 256, 384, zt, 4 * 192, 4 * C)
+        layer(r, 256, 0)
+        for b in range(4):
+            act(T["bp%d" % r][:, C * b + CROSS:C * b + C], T.ps[:, 512 * b + 64:512 * b + 128], ACT.Copy,
+                [bank(b)], [("bp%d" % r, C * b + CROSS, C * b + C)], scale=0.03125)
+        turn("gg", nr, HALF)
+        wrapped("kof%d" % (r + 1), 0, 2, 0, 1.0, 160.0)
+        if r + 1 < ROUNDS:
+            k4 = "k4%d" % (r + 1)
+            for t in range(4):
+                wrapped(k4, 32 * t, 2, 0, 4.0, 640.0 + t)
+            dma("s", "dk%d" % (r + 1), [(T["lk%d" % (r + 1)][:, :], T.gg[0:128:16, nr + 16:nr + 336],
+                                         [("gg", nr + 16, nr + 336)], [("lk%d" % (r + 1), 0, 160)])])
+            share(r + 1)
+            fetch(r + 1)
+        else:
+            tts(T.kpf[:], T.gg[:, nr + 16:nr + 336], 160.0, None, A.add, None, [("gg", nr + 16, nr + 336)], [("kpf", 0, C)])
+            dma("s", "okp", [(T.kp[:, :], T.kpf[0:128:16, :], [("kpf", 0, C)], [])])
+            quant("vq", "vs", 0, 128, "vb", 0, 512)
+        if r == 0:
+            quant("eq", "ep", 0, 512, "eb", 0, 2048)
+        unpack(r, 0, 4)
+        unpack(r, 1, 0)
+        n = r + 1
+        advance(r, 0, range(4))
+        advance(r, 1, [0])
+        if n < ROUNDS:
+            qstate(n, 0)
+            score(n, 0)
+            advance(r, 1, [1, 2, 3])
+            qstate(n, 1)
+            score(n, 1)
+            sign(0)
+            sign(1)
+        else:
+            for i in range(2):
+                a, b = PARTS[i]
+                if i == 1:
+                    advance(r, 1, [1, 2, 3])
+                qstate(n, i)
+                mul(4 + i, b - a, "vq", "vs", 0, "xq%d" % n, "xs%d" % n, a, b)
+                act(T.yo[:, a:b], T.ps[:, 512 * (4 + i):512 * (4 + i) + b - a], ACT.Copy, [bank(4 + i)], [("yo", a, b)])
+                dma("s", "oc%d" % i, [(T.oc[:, 4 * a:4 * b], T["xq%d" % n][:, a:b].bitcast(dt.uint8), [("xq%d" % n, a, b)], [])])
+                dma("a", "oy%d" % i, [(T.y[:, a:b], T.yo[:, a:b], [("yo", a, b)], [])])
+            dma("s", "os", [(T.osc[4 * i:4 * i + 4, :], T["xs%d" % n][32 * i:32 * i + 4, :], [("xs%d" % n, 0, C)], []) for i in range(4)])
+    for sem in total:
+        if seen["g"].get(sem, 0) < total[sem]:
+            g.wait_ge(T.sem[sem], total[sem])

@@ -3,66 +3,59 @@ from concourse.mybir import dt, AluOpType, ActivationFunctionType
 C, HALF, CROSS = 320, 160, 256
 ROUNDS = 3
 MASKS = [1, 2, 3]
-LONG = [(0, 2), (4, 8), (11, 12), (14, 20)]
-SHORT = [(2, 4), (8, 11), (12, 14)]
-BLOCKS = [b for a, e in LONG + SHORT for b in range(a, e)]
-AT = {b: i for i, b in enumerate(BLOCKS)}
-NB = sum(e - a for a, e in LONG)
-NL, NS = 16 * NB, C - 16 * NB
-RADIX = [3, 3, 3, 3, 3]
-BIG, LESS = 1024.0, 256
-G0 = NL + 16
+LEVELS = [[(4, 1, 2), (14, 1, 2)], [(2, 5, 4)], [(3, 10, 2)], [(1, 15, 2)], [(18, 1, 1)]]
+STOPS = [(0, 6, 2), (8, 1, 4), (19, 1, 1)]
+RUNS = LEVELS[1] + LEVELS[2] + LEVELS[3] + LEVELS[4] + STOPS + LEVELS[0]
+ORDER = [b + s * i for b, s, n in RUNS for i in range(n)]
+AT = {b: i for i, b in enumerate(ORDER)}
+NL, NF, N1 = 144, 112, 64
+RADIX = [4, 3, 3, 3]
+BIG, MID, TINY = 1024.0, 168, 2.0 ** -93
+T0 = 16 + NL + NF
+FAR, CH = 192, 416
+G, F0 = 352, 16 + NL
+PARTS = [(0, 192), (192, C)]
+HP = C + 16
 F32, BF, I32, U16, F8, U8 = "float32", "bfloat16", "int32", "uint16", "float8_e4m3fn_x4", "uint8"
 
+
+def table_at(i):
+    return i + 11 if i < 9 else i - 5 if i < 16 else i - 16
+
+
+def _sb(n, kind):
+    return ("sbuf", [128, n], kind)
+
+
 SCRATCH = {
-    "ub": ("sbuf", [128, 512], BF), "vb": ("sbuf", [128, 512], BF),
-    "uq": ("sbuf", [128, 128], F8), "us": ("sbuf", [128, 128], U8),
-    "vq": ("sbuf", [128, 128], F8), "vs": ("sbuf", [128, 128], U8),
-    "wq": ("sbuf", [128, 512], F8), "wp": ("sbuf", [128, 512], U8),
-    "one": ("sbuf", [128, 512], BF), "eb": ("sbuf", [128, 2048], BF),
-    "eq": ("sbuf", [128, 512], F8), "ep": ("sbuf", [128, 512], U8),
-    "pidx": ("sbuf", [128, 1], I32), "qidx": ("sbuf", [128, 1], I32), "grp": ("sbuf", [128, 1], I32),
-    "yrow": ("sbuf", [128, C], F32), "cwi": ("sbuf", [128, 16], F32), "cst": ("sbuf", [128, 16], F32), "sel": ("sbuf", [128, 12], U16),
-    "rt": ("sbuf", [128, 128], F32), "ru": ("sbuf", [128, 128], F32), "ki": ("sbuf", [128, 5], I32), "kf": ("sbuf", [128, 5], F32),
-    "dr": ("sbuf", [128, HALF], F32), "d1": ("sbuf", [128, HALF], F32), "k1b": ("sbuf", [128, HALF], F32), "k3b": ("sbuf", [128, HALF], F32),
-    "k1": ("sbuf", [128, HALF], BF), "k3": ("sbuf", [128, HALF], F32), "bs0": ("sbuf", [128, NL], BF),
-    "cw": ("sbuf", [128, 16], F32), "ca": ("sbuf", [128, 16], F32), "cb": ("sbuf", [128, 16], F32), "cd": ("sbuf", [128, 16], F32),
-    "c2": ("sbuf", [128, 16], F32), "ct0": ("sbuf", [128, 16], F32), "ct1": ("sbuf", [128, 16], F32),
-    "dl": ("sbuf", [128, 64], F32), "dat": ("sbuf", [128, 64], F32), "sc": ("sbuf", [128, 64], F32),
-    "fi": ("sbuf", [128, 16], I32), "fa": ("sbuf", [128, 16], I32),
-    "kli": ("sbuf", [128, 20], I32), "klb": ("sbuf", [128, 32], BF), "klt": ("sbuf", [128, 32], BF),
-    "w0": ("sbuf", [128, G0 + C + 16], BF), "gg": ("sbuf", [128, 5 * 352], BF), "krs": ("sbuf", [128, 3 * C], BF),
-    "bits": ("sbuf", [128, C], BF), "bs1": ("sbuf", [128, NL], BF), "bs2": ("sbuf", [128, NL], BF),
-    "tt": ("sbuf", [128, 864], BF), "of0": ("sbuf", [128, 16], U16), "of1": ("sbuf", [128, 16], U16), "ofs": ("sbuf", [128, 16], U16),
-    "kpf": ("sbuf", [128, C], F32), "yo": ("sbuf", [128, C], F32),
+    "ub": _sb(512, BF), "vb": _sb(512, BF), "uq": _sb(128, F8), "us": _sb(128, U8), "vq": _sb(128, F8), "vs": _sb(128, U8),
+    "wq": _sb(512, F8), "wp": _sb(512, U8), "one": _sb(512, BF), "eb": _sb(2048, BF), "eq": _sb(512, F8), "ep": _sb(512, U8),
+    "pidx": _sb(1, I32), "qidx": _sb(1, I32), "grp": _sb(1, I32), "par": _sb(1, I32), "q8": _sb(1, I32),
+    "yrow": _sb(C, F32), "ym": _sb(C, BF), "cst": _sb(16, F32), "sel": _sb(12, U16), "rowc": _sb(112, BF), "lst": _sb(16, F32),
+    "ki": _sb(2, I32), "kj": _sb(2, I32), "kf": _sb(2, F32), "tab": _sb(32, F32), "tbm": _sb(40, F32), "pu": _sb(20, U16), "p8": _sb(20, U16),
+    "p4": _sb(C, F32), "sb": _sb(C, F32), "bs0": _sb(NL + NF, BF), "bs1": _sb(NF, BF), "bs2": _sb(NF, BF),
+    "cw": _sb(16, F32), "ca": _sb(16, F32), "cb": _sb(16, F32), "cd": _sb(16, F32), "ce": _sb(16, F32),
+    "c2": _sb(16, F32), "ct0": _sb(16, F32), "ct1": _sb(16, F32),
+    "dl": _sb(96, F32), "dat": _sb(96, F32), "sc": _sb(64, F32), "fi": _sb(16, I32), "fa": _sb(16, I32),
+    "eo": _sb(32, F32), "ed": _sb(16, F32), "kli": _sb(20, I32), "kw": _sb(32, F32), "kpi": _sb(32, U16), "k4": _sb(128, U16),
+    "w0": _sb(T0 + 336, BF), "gg": _sb(2 * G, BF), "bits": _sb(2 * C, BF), "ta": _sb(2 * CH, BF), "tb": _sb(CH, BF),
+    "ofa": _sb(16, U16), "ofb": _sb(16, U16), "ofc": _sb(2, U16), "ofl": _sb(16, U16), "ofn": _sb(16, U16), "of0": _sb(16, U16), "of1": _sb(16, U16),
+    "kr": _sb(C, BF), "kk": _sb(C, BF), "kd": _sb(400, BF), "tof": _sb(20, U16), "own": _sb(20, U16),
+    "yp": _sb(4 * C, BF), "yi": _sb(4 * C, BF), "zc": _sb(4 * C, BF), "zt": _sb(4 * C, BF), "zq": _sb(384, F8), "zs": _sb(384, U8),
+    "hp": _sb(4 * HP, BF), "ht": _sb(4 * C, BF), "xp": _sb(4 * C, BF),
+    "xq": _sb(C, F8), "xs": _sb(C, U8), "kpf": _sb(C, F32), "yo": _sb(C, F32),
     "ps": ("psum", [128, 4096], F32),
 }
 for _r in range(ROUNDS + 1):
-    SCRATCH["xt%d" % _r] = ("sbuf", [128, 4 * C], BF)
-    SCRATCH["xq%d" % _r] = ("sbuf", [128, C], F8)
-    SCRATCH["xs%d" % _r] = ("sbuf", [128, C], U8)
-    SCRATCH["kof%d" % _r] = ("sbuf", [128, 32], U16)
+    SCRATCH["xt%d" % _r] = _sb(4 * C, BF)
+    SCRATCH["kof%d" % _r] = _sb(20, U16)
 for _r in range(ROUNDS):
-    SCRATCH["k4%d" % _r] = ("sbuf", [128, 128], U16)
-    SCRATCH["tof%d" % _r] = ("sbuf", [128, 20], U16)
-    SCRATCH["kk%d" % _r] = ("sbuf", [128, C], BF)
-    SCRATCH["yp%d" % _r] = ("sbuf", [128, 4 * C], BF)
-    SCRATCH["yi%d" % _r] = ("sbuf", [128, 4 * C], BF)
-    SCRATCH["zt%d" % _r] = ("sbuf", [128, 4 * C], BF)
-    SCRATCH["zq%d" % _r] = ("sbuf", [128, 384], F8)
-    SCRATCH["zs%d" % _r] = ("sbuf", [128, 384], U8)
-    SCRATCH["ht%d" % _r] = ("sbuf", [128, 4 * CROSS], BF)
-    SCRATCH["hq%d" % _r] = ("sbuf", [128, CROSS], F8)
-    SCRATCH["hs%d" % _r] = ("sbuf", [128, CROSS], U8)
-    SCRATCH["rq%d" % _r] = ("sbuf", [128, CROSS], F8)
-    SCRATCH["rs%d" % _r] = ("sbuf", [128, CROSS], U8)
-    SCRATCH["bp%d" % _r] = ("sbuf", [128, 4 * C], BF)
-    SCRATCH["lk%d" % _r] = ("dram", [128, 20], BF)
-    SCRATCH["rk%d" % _r] = ("dram", [128, 20], BF)
+    for _n, _k, _w in (("hq", F8, C), ("hs", U8, C), ("rq", F8, C), ("rs", U8, C), ("nm", U16, 20), ("rn", U16, 20), ("rk", U16, 20)):
+        SCRATCH["%s%d" % (_n, _r)] = _sb(_w, _k)
 SEMAPHORES = ["sv", "sa", "sp", "sg", "sent", "lx0", "lx1", "lu", "lv", "lk", "lwc", "lws",
               "oc0", "oc1", "os", "oy0", "oy1", "okp"]
 for _r in range(ROUNDS):
-    SEMAPHORES += ["dk%d" % _r, "dr%d" % _r, "arl%d" % _r, "ar0%d" % _r, "ar1%d" % _r]
+    SEMAPHORES += ["ark%d" % _r, "arn%d" % _r, "ar0%d" % _r, "ar1%d" % _r]
 
 
 def rank_program(g, core, T, topo):
@@ -71,17 +64,32 @@ def rank_program(g, core, T, topo):
         return
     A, ACT = AluOpType, ActivationFunctionType
     queue = {"v": g.vector, "a": g.scalar, "p": g.tensor, "g": g, "s": g.sync}
-    own = {"v": "sv", "a": "sa", "p": "sp", "g": "sg"}
+    mine = {"v": "sv", "a": "sa", "p": "sp", "g": "sg"}
     total, seen, hist = {}, {q: {} for q in queue}, {}
 
-    def need(q, reads, writes, compute):
+    def V(nm, a=0, b=None, step=1):
+        b = SCRATCH[nm][1][1] if b is None else b
+        cols = range(512 * (a // 512), 512 * (a // 512) + 512) if nm == "ps" else range(a, b, step)
+        return (T[nm][:, a:b:step] if step > 1 else T[nm][:, a:b], [(nm, sum(1 << c for c in cols))])
+
+    def by(win, off):
+        return (win[0].indirect(off[0]), win[1] + off[1])
+
+    def raw(v):
+        return (v[0].bitcast(dt.uint8), v[1])
+
+    def ap(x):
+        return x[0] if isinstance(x, tuple) else x
+
+    def feet(xs):
+        return [f for x in xs if isinstance(x, tuple) for f in x[1]]
+
+    def need(q, reads, writes):
         deps = {}
-        for (names, isw) in ((reads, False), (writes, True)):
-            for (b, lo, hi) in names:
-                for (l, h, w, eq, sem, val) in hist.get(b, []):
-                    if l < hi and lo < h and (w or isw):
-                        if compute and eq == q and isw:
-                            continue
+        for names, isw in ((reads, False), (writes, True)):
+            for b, m in names:
+                for (em, w, eq, sem, val) in hist.get(b, []):
+                    if em & m and (w or isw or (b == "ps" and eq != q)):
                         deps[sem] = max(deps.get(sem, 0), val)
         for sem in deps:
             if seen[q].get(sem, 0) < deps[sem]:
@@ -89,428 +97,431 @@ def rank_program(g, core, T, topo):
                 seen[q][sem] = deps[sem]
 
     def note(q, reads, writes, sem, val):
-        for (b, lo, hi) in writes:
-            hist[b] = [e for e in hist.get(b, []) if not (lo <= e[0] and e[1] <= hi and (e[3] != q or e[2] is False or (lo, hi) == (e[0], e[1])))]
-            hist[b].append((lo, hi, True, q, sem, val))
-        for (b, lo, hi) in reads:
-            keep = [e for e in hist.get(b, []) if not (not e[2] and e[3] == q and lo <= e[0] and e[1] <= hi)]
-            keep.append((lo, hi, False, q, sem, val))
-            hist[b] = keep
+        for b, m in writes:
+            hist[b] = [e for e in hist.get(b, []) if e[0] & ~m] + [(m, True, q, sem, val)]
+        for b, m in reads:
+            hist[b] = [e for e in hist.get(b, []) if e[1] or e[3] != sem or e[0] & ~m] + [(m, False, q, sem, val)]
 
-    def op(q, call, reads, writes):
-        need(q, reads, writes, True)
-        sem = own[q]
-        total[sem] = total.get(sem, 0) + 1
-        call(queue[q]).then_inc(T.sem[sem], 1)
-        note(q, reads, writes, sem, total[sem])
+    def op(q, call, out, *ins):
+        reads, writes = feet(ins), out[1]
+        need(q, reads, writes)
+        total[mine[q]] = total.get(mine[q], 0) + 1
+        call(queue[q]).then_inc(T.sem[mine[q]], 1)
+        note(q, reads, writes, mine[q], total[mine[q]])
 
     def dma(q, sem, pairs):
-        for (out, in_, reads, writes) in pairs:
-            need(q, reads, writes, False)
-        for (out, in_, reads, writes) in pairs:
+        for out, in_ in pairs:
+            need(q, feet([in_]), feet([out]))
+        for out, in_ in pairs:
             total[sem] = total.get(sem, 0) + 16
-            queue[q].dma_start(out, in_).then_inc(T.sem[sem], 16)
-        for (out, in_, reads, writes) in pairs:
-            note("d" + q, reads, writes, sem, total[sem])
+            queue[q].dma_start(ap(out), ap(in_)).then_inc(T.sem[sem], 16)
+        for out, in_ in pairs:
+            note("d" + q, feet([in_]), feet([out]), sem, total[sem])
 
-    def send(dst, out, in_, reads, sem):
-        need("g", reads, [], False)
+    def send(dst, out, in_, sem):
+        need("g", in_[1], [])
         rid, pid = topo.addr(dst)[0], topo.addr(dst)[1]
         n = len(topo.engines(core, dst))
-        g.remote_dma(out, in_, T.sem[sem], T.sem.sent, pid, rid, topo.mask(core, dst))
+        g.remote_dma(out[0], in_[0], T.sem[sem], T.sem.sent, pid, rid, topo.mask(core, dst))
         total["sent"] = total.get("sent", 0) + n
         total[sem] = total.get(sem, 0) + n
 
-    def tts(out, in0, s1, s2, o0, o1, reads, writes):
-        if o1 is None:
-            op("v", lambda e: e.tensor_scalar(out, in0, s1, None, o0), reads, writes)
-        else:
-            op("v", lambda e: e.tensor_scalar(out, in0, s1, s2, o0, o1), reads, writes)
+    def landed(sem, *views):
+        note("net", [], feet(views), sem, total[sem])
 
-    def ttt(out, in0, in1, o, reads, writes):
-        op("v", lambda e: e.tensor_tensor(out, in0, in1, o), reads, writes)
+    def tts(out, in0, s1, o0, s2=None, o1=None):
+        tail = (o0,) if o1 is None else (o0, o1)
+        op("v", lambda e: e.tensor_scalar(out[0], in0[0], ap(s1), ap(s2), *tail), out, in0, s1, s2)
 
-    def act(out, in_, f, reads, writes, **k):
-        op("a", lambda e: e.activation(out, in_, f, **k), reads, writes)
+    def ttt(out, in0, in1, o):
+        op("v", lambda e: e.tensor_tensor(out[0], in0[0], in1[0], o), out, in0, in1)
 
-    def quant(q, s, a, b, t, ta, tb):
-        op("v", lambda e: e.quantize_mx(T[q][:, a:b], T[s][:, a:b], T[t][:, ta:tb]), [(t, ta, tb)], [(q, a, b), (s, a, b)])
+    def fill(out, x):
+        op("v", lambda e: e.memset(out[0], x), out)
 
-    def bank(i):
-        return ("ps", 512 * i, 512 * i + 512)
+    def act(out, in_, f=ACT.Copy, **k):
+        op("a", lambda e: e.activation(out[0], in_[0], f, **{n: ap(k[n]) for n in k}), out, in_, *k.values())
 
-    def mul(i, n, lq, ls, l, rq, rs, a, b):
-        op("p", lambda e: e.matmul_mx(T.ps[:, 512 * i:512 * i + n], T[lq][:, l:l + 128], T[ls][:, l:l + 128],
-                                      T[rq][:, a:b], T[rs][:, a:b], True, True),
-           [(lq, l, l + 128), (ls, l, l + 128), (rq, a, b), (rs, a, b)], [bank(i)])
+    def iota(out, pattern, base, mult, **k):
+        op("g", lambda e: e.iota(out[0], pattern, base, mult, **k), out)
 
-    peer = [T.cores[rank ^ m] for m in MASKS]
-    dma("s", "lx0", [(T.xt0[:, 0:768], T.x[:, 0:768], [], [("xt0", 0, 768)])])
-    dma("a", "lk", [(T.kli[:], T.kl[:, :], [], [("kli", 0, 20)])])
-    dma("s", "lx1", [(T.xt0[:, 768:1280], T.x[:, 768:1280], [], [("xt0", 768, 1280)])])
-    dma("a", "lu", [(T.ub[:], T.u[:, :], [], [("ub", 0, 512)])])
-    dma("s", "lwc", [(T.wq[:, 0:512].bitcast(dt.uint8), T.wc[:, 0:2048], [], [("wq", 0, 512)])])
-    dma("s", "lws", [(T.wp[:, 0:512], T.ws[:, 0:512], [], [("wp", 0, 512)])])
-    dma("a", "lv", [(T.vb[:], T.v[:, :], [], [("vb", 0, 512)])])
+    def quant(q, s, a, b, t, ta):
+        qv, sv, tv = V(q, a, b), V(s, a, b), V(t, 4 * ta, 4 * (ta + b - a))
+        op("v", lambda e: e.quantize_mx(qv[0], sv[0], tv[0]), (None, qv[1] + sv[1]), tv)
+
+    def bank(i, a, b):
+        return V("ps", 512 * i + a, 512 * i + b)
+
+    def mul(i, lq, ls, l, rq, rs, a, b):
+        x = [V(lq, l, l + 128), V(ls, l, l + 128), V(rq, a, b), V(rs, a, b)]
+        out = bank(i, 0, b - a)
+        op("p", lambda e: e.matmul_mx(out[0], x[0][0], x[1][0], x[2][0], x[3][0], True, True), out, *x)
+
+    def flip(out, in_):
+        op("v", lambda e: e.transpose(out[0], in_[0]), out, in_)
+
+    def flips(to, at, nm, c, n):
+        n1, n2 = 32 * ((n + 31) // 32), 32 * ((n + 47) // 32)
+        return [lambda: flip(V(to, at, at + n1), V(nm, c, c + n1)), lambda: flip(V(to, at + FAR, at + FAR + n2), V(nm, c - 16, c - 16 + n2))]
+
+    def wrapped(out, to, at, mult, plus, chunks=1):
+        tts(out, by(V(to, at, at + chunks * CH), V("sel", 0, chunks)), mult, A.mult, plus, A.add)
+
+    def run(calls):
+        for call in calls:
+            call()
 
     later = []
 
-    def drip(n):
-        for call in later[:n]:
-            call()
+    def drip(n=1):
+        now = later[:n]
         later[:n] = []
+        run(now)
 
     def col(i):
-        return T.cst[:, i:i + 1]
+        return V("cst", i, i + 1)
 
-    def cc(*i):
-        return [("cst", j, j + 1) for j in i]
+    peer = [T.cores[rank ^ m] for m in MASKS]
+    dma("s", "lx0", [(V("xt0", 0, 768), T.x[:, 0:768])])
+    dma("a", "lk", [(V("kli"), T.kl[:, :])])
+    dma("s", "lx1", [(V("xt0", 768, 1280), T.x[:, 768:1280])])
+    dma("a", "lu", [(V("ub"), T.u[:, :])])
+    dma("s", "lwc", [(raw(V("wq")), T.wc[:, 0:2048])])
+    dma("s", "lws", [(V("wp"), T.ws[:, 0:512])])
+    dma("a", "lv", [(V("vb"), T.v[:, :])])
 
-    def scol(i, in0, names, s1, s2, o0, o1):
-        tts(col(i), in0, s1, s2, o0, o1, names, cc(i))
-    P1, Q1, GR, YR = ("pidx", 0, 1), ("qidx", 0, 1), ("grp", 0, 1), ("yrow", 0, C)
-    op("g", lambda e: e.iota(T.pidx[:], [[0, 1]], 0, 1), [], [P1])
-    op("g", lambda e: e.iota(T.yrow[:], [[1, C]], 0, 0, allow_small_or_imprecise_dtypes=True), [], [YR])
-    op("g", lambda e: e.iota(T.cwi[:], [[16, 16]], 0, 1, allow_small_or_imprecise_dtypes=True), [], [("cwi", 0, 16)])
-    op("v", lambda e: e.memset(T.rt[:], 0.0), [], [("rt", 0, 128)])
-    op("v", lambda e: e.memset(T.one[:], 1.0), [], [("one", 0, 512)])
-    op("v", lambda e: e.memset(T.klb[:], 0.0), [], [("klb", 0, 32)])
-    cuts = sorted([(a, e, 16 * (AT[a] - a)) for a, e in LONG] + [(a, e, G0) for a, e in SHORT])
-    for a, e, d in cuts:
-        op("v", lambda x: x.memset(T.dr[:, 8 * a:8 * e], float(d)), [], [("dr", 8 * a, 8 * e)])
-    tts(T.qidx[:], T.pidx[:], 15, None, A.bitwise_and, None, [P1], [Q1])
-    tts(T.grp[:], T.pidx[:], 4, None, A.arith_shift_right, None, [P1], [GR])
-    scol(0, T.qidx[:], [Q1], 0.0, None, A.is_equal, None)
-    scol(1, T.qidx[:], [Q1], 0.0, BIG, A.is_equal, A.mult)
-    scol(8, T.grp[:], [GR], 1.0, None, A.mult, None)
-    scol(9, T.grp[:], [GR], 16.0, None, A.mult, None)
-    scol(2, col(0), cc(0), 1.0, None, A.add, None)
-    scol(3, col(0), cc(0), float(-LESS), None, A.mult, None)
-    scol(4, col(0), cc(0), 2.0, 2.0, A.mult, A.add)
-    scol(5, col(0), cc(0), float(1 - 2 * LESS - HALF), float(HALF), A.mult, A.add)
-    scol(6, col(0), cc(0), -LESS - BIG, BIG, A.mult, A.add)
-
-    def widen(nm, a, b, src, c, scale, bias, names):
-        act(T[nm][:, a:b], T[src][:, c:c + b - a], ACT.Identity, [(src, c, c + b - a)] + names, [(nm, a, b)], bias=bias, scale=scale)
+    small = {"allow_small_or_imprecise_dtypes": True}
+    Q, GR = V("qidx"), V("grp")
+    iota(V("pidx"), [[0, 1]], 0, 1)
+    iota(V("yrow"), [[1, C]], 0, 0, **small)
+    for b, s, n in RUNS:
+        iota(V("tab", b, b + s * (n - 1) + 1, s), [[32 * (1 - s), n]], 32 * (table_at(AT[b]) - b) - 2 * MID, 0, **small)
+    fill(V("one"), 1.0)
+    fill(V("rowc"), 0.0)
+    fill(V("kw"), 0.0)
+    tts(Q, V("pidx"), 15, A.bitwise_and)
+    tts(GR, V("pidx"), 4, A.arith_shift_right)
+    tts(V("q8"), V("pidx"), 3, A.arith_shift_right, 1, A.bitwise_and)
+    tts(col(0), Q, 0.0, A.is_equal)
+    tts(col(5), GR, 1.0, A.mult)
+    tts(col(9), Q, 1.0, A.mult)
+    tts(col(10), Q, 11.0, A.min, 16.0, A.mult)
+    tts(col(11), V("q8"), 1.0, A.mult)
+    tts(V("par"), Q, col(5), A.add)
+    tts(col(7), col(0), 3.0, A.mult, 1.0, A.add)
+    tts(V("par"), V("par"), 1, A.bitwise_and)
+    tts(col(1), col(0), BIG, A.mult)
+    tts(col(2), col(0), 2.0, A.mult)
+    tts(V("sel", 0, 1), V("par"), float(FAR + 16), A.mult, col(10), A.add)
 
     def blank(nm, a, b):
-        act(T[nm][:, a:b], T.yrow[:, 0:b - a], ACT.Copy, [YR], [(nm, a, b)], scale=0.0)
-    lists = [LONG, SHORT]
-    for h in (0, 10):
-        runs = []
-        for b in range(h, h + 10):
-            if runs and AT[b] == runs[-1][1]:
-                runs[-1][1] += 1
-            else:
-                runs.append([AT[b], AT[b] + 1])
-        lists.append(runs)
+        for c in range(a, b, 512):
+            act(V(nm, c, min(b, c + 512)), V("one", 0, min(b - c, 512)), scale=0.0)
+    blank("tb", 0, CH)
+    blank("ta", 0, 2 * CH)
+    for b, s, n in RUNS:
+        tts(V("rowc", 64 + AT[b], 64 + AT[b] + n), V("yrow", 0, n), float(s), A.mult, float(b), A.add)
+    tts(V("pu"), V("rowc", 64, 84), 16.0, A.mult, col(9), A.add)
+    tts(V("p8"), V("rowc", 64, 84), 2.0, A.mult, col(11), A.add)
+    act(V("p4"), by(V("yrow"), V("pu")), ACT.Identity, scale=col(7))
+    blank("gg", F0 + NF, G + F0)
+    blank("gg", G + F0 + NF, 2 * G)
+    act(V("ym"), V("yrow"), ACT.Identity, bias=-160.0)
+    blank("w0", 0, 16)
+    run(flips("tb", 0, "rowc", 64, 32))
+    tts(col(3), col(0), -1.0, A.mult)
+    tts(col(4), col(0), TINY, A.mult)
+    tts(col(12), col(0), -TINY, A.mult)
+    wrapped(V("lst"), "tb", 0, 1.0, 0.0)
+    tts(V("kof0"), V("kli"), 0.0, A.add)
+    tts(V("tbm", 0, 20), V("tab", 0, 20), 1.0, A.add, col(0), A.mult)
+    tts(V("tbm", 20, 40), V("tab", 0, 20), float(1 - 2 * C), A.add, col(0), A.mult)
+    tts(col(8), col(0), 32.0 * (20 - table_at(AT[0])), A.mult)
+    tts(col(6), col(0), 2.0 * (N1 - MID) - BIG, A.mult, BIG, A.add)
 
-    def row_of(i):
-        for j in (32 * i, 32 * i + 16):
-            for a, e in lists[i]:
-                w = ("rt", j, j + e - a)
-                if i < 2:
-                    act(T.rt[:, j:j + e - a], T.yrow[:, a:e], ACT.Copy, [YR, w], [w])
-                else:
-                    op("g", lambda x: x.iota(T.rt[:, j:j + e - a], [[1, e - a]], a, 0, allow_small_or_imprecise_dtypes=True), [w], [w])
-                j += e - a
-    row_of(2)
-    row_of(3)
-    widen("k1b", 0, HALF, "yrow", 0, col(2), col(3), cc(2, 3))
-    widen("d1", 0, HALF, "dr", 0, col(0), 0.0, cc(0))
-    widen("k3b", 0, HALF, "yrow", 0, col(4), col(5), cc(4, 5))
-    row_of(0)
-    row_of(1)
-    blank("tt", 672, 864)
-    ttt(T.k1[:], T.k1b[:], T.d1[:], A.add, [("k1b", 0, HALF), ("d1", 0, HALF)], [("k1", 0, HALF)])
-    tts(T.d1[:], T.d1[:], 2.0, None, A.mult, None, [("d1", 0, HALF)], [("d1", 0, HALF)])
-    KL = [("kli", 0, 20)]
-    tts(T.klb[:, 0:20], T.kli[:], -160.0, None, A.add, None, KL, [("klb", 0, 20)])
-    tts(T.kof0[:, 0:20], T.kli[:], 0.0, None, A.add, None, KL, [("kof0", 0, 20)])
-    ttt(T.k3[:], T.k3b[:], T.d1[:], A.add, [("k3b", 0, HALF), ("d1", 0, HALF)], [("k3", 0, HALF)])
-    op("v", lambda e: e.transpose(T.klt[:], T.klb[:]), [("klb", 0, 32)], [("klt", 0, 32)])
-    WIDE = 32 * ((NB + 1) // 2)
-    RU, KI, KF = [("ru", 0, 128)], [("ki", 0, 4)], [("kf", 0, 4)]
-    KQ = [("ki", 4, 5), ("kf", 4, 5)]
-
-    def seln(o, in0, s1, s2, o0, o1, names):
-        tts(o, in0, s1, s2, o0, o1, names, [("sel", 0, 12)])
-    tts(T.ki[:, 4:5], T.qidx[:], col(8), None, A.add, None, [Q1] + cc(8), [("ki", 4, 5)])
-    tts(T.kf[:, 4:5], T.qidx[:], 16.0, None, A.mult, None, [Q1], [("kf", 4, 5)])
-
-    def own_places():
-        tts(T.ki[:, 4:5], T.ki[:, 4:5], 1, None, A.bitwise_and, None, [("ki", 4, 5)], [("ki", 4, 5)])
-        for t in range(4):
-            tts(T.k40[:, 32 * t:32 * t + 20], T.kli[:], 4.0, float(t), A.mult, A.add, KL, [("k40", 32 * t, 32 * t + 20)])
-        seln(T.sel[:, 6:7], T.ki[:, 4:5], float(WIDE + 16), T.kf[:, 4:5], A.mult, A.add, KQ)
-        seln(T.sel[:, 0:1], T.ki[:, 4:5], float(C + 16), T.kf[:, 4:5], A.mult, A.add, KQ)
-
-    where = [
-        lambda: op("v", lambda e: e.transpose(T.ru[:], T.rt[:]), [("rt", 0, 128)], RU),
-        lambda: (tts(T.ki[:, 0:4], T.ru[:, 0:128:32], col(8), None, A.add, None, RU + cc(8), KI),
-                 tts(T.kf[:, 0:4], T.ru[:, 0:128:32], 16.0, None, A.mult, None, RU, KF)),
-        lambda: tts(T.ki[:, 0:4], T.ki[:, 0:4], 1, None, A.bitwise_and, None, KI, KI),
-        lambda: tts(T.ki[:, 0:4], T.ki[:, 0:4], C + 16, None, A.mult, None, KI, KI),
-        lambda: ttt(T.kf[:, 0:4], T.kf[:, 0:4], T.ki[:, 0:4], A.add, KI + KF, KF),
-        lambda: seln(T.sel[:, 2:6:2], T.kf[:, 0:2], 0.0, None, A.add, None, KF)]
-
-    def find(i):
-        where[i]()
-    later += [lambda: seln(T.sel[:, 8:12:2], T.kf[:, 2:4], 1.0, None, A.add, None, KF),
-              lambda: seln(T.sel[:, 1:2], T.sel[:, 0:1], 256.0, None, A.add, None, [("sel", 0, 12)])]
-    SE = ("sel", 0, 12)
-    for a, e in LONG:
-        widen("bs0", 16 * AT[a], 16 * (AT[a] + e - a), "yrow", 16 * a, 1.0, col(1), cc(1))
-    widen("w0", 0, NL, "yrow", 0, col(0), col(6), cc(0, 6))
-    blank("w0", NL, G0)
-    blank("w0", G0 + C, G0 + C + 16)
-    for i in range(2):
-        blank("gg", 352 * i, 352 * i + 16)
-        blank("gg", 352 * i + 16 + NL, 352 * i + 352)
-    CW = [("cw", 0, 16)]
-    later += [
-        lambda: tts(T.cw[:], T.cwi[:], col(9), None, A.subtract, None, [("cwi", 0, 16)] + cc(9), CW),
-        lambda: op("v", lambda e: e.memset(T.dl[:, 0:64:4], 0.0), [], [("dl", 0, 64)]),
-        lambda: tts(T.c2[:], T.cw[:], 2.0, -160.0, A.mult, A.add, CW, [("c2", 0, 16)]),
-        lambda: op("v", lambda e: e.memset(T.dl[:, 3:64:4], -1.0), [], [("dl", 0, 64)]),
-        lambda: tts(T.dat[:, 3:64:4], T.cw[:], 4.0, -319.0, A.mult, A.add, CW, [("dat", 0, 64)]),
-        lambda: tts(T.ca[:], T.cw[:], 0.0, None, A.is_equal, None, CW, [("ca", 0, 16)]),
-        lambda: tts(T.dl[:, 1:64:4], T.cw[:], 159.0, 2.0, A.is_equal, A.mult, CW, [("dl", 0, 64)]),
-        lambda: tts(T.cb[:], T.cw[:], 159.0, -160.0, A.is_equal, A.mult, CW, [("cb", 0, 16)]),
-        lambda: ttt(T.ca[:], T.cw[:], T.ca[:], A.subtract, CW + [("ca", 0, 16)], [("ca", 0, 16)]),
-        lambda: tts(T.dl[:, 1:64:4], T.dl[:, 1:64:4], -1.0, None, A.add, None, [("dl", 0, 64)], [("dl", 0, 64)]),
-        lambda: tts(T.cd[:], T.cw[:], 159.0, 161.0, A.is_equal, A.mult, CW, [("cd", 0, 16)]),
-        lambda: ttt(T.ct0[:], T.ca[:], T.cb[:], A.add, [("ca", 0, 16), ("cb", 0, 16)], [("ct0", 0, 16)]),
-        lambda: ttt(T.ct1[:], T.ca[:], T.cd[:], A.add, [("ca", 0, 16), ("cd", 0, 16)], [("ct1", 0, 16)])]
-
-    dma("s", "dk0", [(T.lk0[16 * i:16 * i + 16, :], T.klt[32 * (i // 2):32 * (i // 2) + 20, 16 * (i % 2):16 * (i % 2) + 16],
-                      [("klt", 0, 32)], [("lk0", 20 * i, 20 * i + 20)]) for i in range(8)])
+    def scores_list(k):
+        return [lambda: tts(V("kw", 0, 10), V(k, 0, 10), 0.0, A.add), lambda: tts(V("kw", 10, 20), V(k, 0, 10), float(C), A.add),
+                lambda: tts(V("kpi"), by(V("kw"), V("sel", 2, 4)), 0.0, A.add)]
 
     def share(r):
-        send(peer[r], T["rk%d" % r][:, :], T["lk%d" % r][:, :], [("lk%d" % r, 0, 160)], "arl%d" % r)
-        note("net", [], [("rk%d" % r, 0, 160)], "arl%d" % r, total["arl%d" % r])
-
-    def fetch(r):
-        dma("s", "dr%d" % r, [(T.krs[0:128:16, C * r:C * r + C], T["rk%d" % r][:, :],
-                               [("rk%d" % r, 0, 160)], [("krs", C * r, C * r + C)])])
+        send(peer[r], V("rk%d" % r), V("kof%d" % r), "ark%d" % r)
+        landed("ark%d" % r, V("rk%d" % r))
 
     share(0)
+    iota(V("kd"), [[0, 400]], 0, 0, **small)
+    for t in range(4):
+        iota(V("zc", C * t + 192, C * t + CROSS), [[0, 64]], 0, 0, **small)
+        iota(V("hp", HP * t + CROSS, HP * t + CROSS + 16), [[0, 16]], 0, 0, **small)
     for b in range(4):
         op("g", lambda e: e.affine_select(T.eb[:, 512 * b:512 * b + 512], T.one[:], [[1, 512]], A.is_equal, 0.0, -b, -4),
-           [("one", 0, 512)], [("eb", 512 * b, 512 * b + 512)])
+           V("eb", 512 * b, 512 * b + 512), V("one"))
+    LH = V("lst", 0, 4, 2)
+    CW = V("cw")
+    second = [
+        lambda: tts(V("rowc", 48, 64), V("rowc", 26, 42), 0.0, A.add),
+        lambda: run(flips("tb", 0, "rowc", 16, 48)),
+        lambda: wrapped(V("lst"), "tb", 0, 1.0, 0.0),
+        lambda: (tts(V("ki"), LH, col(5), A.add), tts(V("c2"), CW, 2.0, A.mult, -160.0, A.add)),
+        lambda: (tts(V("kj"), V("ki"), 1, A.bitwise_and), fill(V("dl"), -1.0)),
+        lambda: tts(V("kf"), V("kj"), float(FAR // 16 + 1), A.mult),
+        lambda: ttt(V("kf"), V("kf"), LH, A.add)]
+    rest = [
+        lambda: tts(V("sel", 4, 5), V("kf", 0, 1), 16.0, A.mult),
+        lambda: tts(V("sel", 6, 10, 2), V("kf"), 16.0, A.mult, 1.0, A.add),
+        lambda: tts(V("sel", 1, 2), V("sel", 0, 1), float(CH), A.add),
+        lambda: tts(V("dat", 3, 96, 6), CW, 4.0, A.mult, -319.0, A.add),
+        lambda: fill(V("dl", 0, 96, 6), 0.0),
+        lambda: tts(V("ca"), CW, 0.0, A.is_equal),
+        lambda: tts(V("ce"), CW, 159.0, A.is_equal, 2.0, A.mult),
+        lambda: tts(V("cb"), CW, 159.0, A.is_equal, -160.0, A.mult),
+        lambda: ttt(V("ca"), CW, V("ca"), A.subtract),
+        lambda: tts(V("dl", 1, 96, 6), V("ce"), -1.0, A.add),
+        lambda: tts(V("cd"), CW, 159.0, A.is_equal, 161.0, A.mult),
+        lambda: ttt(V("ct0"), V("ca"), V("cb"), A.add),
+        lambda: ttt(V("ct1"), V("ca"), V("cd"), A.add)]
 
-    def flip(to, nm, c, n):
-        op("v", lambda e: e.transpose(T.tt[:, to:to + n], T[nm][:, c:c + n]), [(nm, c, c + n)], [("tt", to, to + n)])
-
-    def turn(nm, c0, cut, ahead=None, between=None):
-        if ahead is not None:
-            ahead()
-        flip(0, nm, c0 + 16, cut)
-        flip(C, nm, c0, cut)
-        if between is not None:
-            between()
-        flip(cut, nm, c0 + 16 + cut, C - cut)
-        flip(C + cut, nm, c0 + cut, C + 32 - cut)
-
-    TT, TN = T.tt[:, 0:864], ("tt", 0, 864)
-
-    def wrapped(nm, a, wide, sel, by, plus):
-        tts(T[nm][:, a:a + 16 * wide], TT.indirect(T.sel[:, sel:sel + wide]), by, plus, A.mult, A.add,
-            [TN, SE], [(nm, a, a + 16 * wide)])
-
-    PARTS = [(0, 192), (192, C)]
-
-    def qstate(r, i):
+    def scores(r, i):
         a, b = PARTS[i]
-        quant("xq%d" % r, "xs%d" % r, a, b, "xt%d" % r, 4 * a, 4 * b)
+        quant("xq", "xs", a, b, "xt%d" % r, a)
+        mul(i, "uq", "us", 0, "xq", "xs", a, b)
+        act(V("bits", a, b), bank(i, 0, b - a), ACT.Sign, scale=col(0), bias=col(12))
+        act(V("bits", C + a, C + b), bank(i, 0, b - a), ACT.Sign, scale=col(3), bias=col(4))
 
-    def score(r, i):
-        a, b = PARTS[i]
-        mul(4 + i, b - a, "uq", "us", 0, "xq%d" % r, "xs%d" % r, a, b)
+    def fours(k):
+        return [lambda t=t: tts(V("k4", 32 * t, 32 * t + 20), V(k), 4.0, A.mult, float(t), A.add) for t in range(4)]
 
-    def sign(i):
-        a, b = PARTS[i]
-        tts(T.bits[:, a:b], T.ps[:, 512 * (4 + i):512 * (4 + i) + b - a], 0.0, col(0), A.is_gt, A.mult, [bank(4 + i)] + cc(0), [("bits", a, b)])
+    calls = scores_list("kli")
+    run(calls[:2])
+    quant("uq", "us", 0, 128, "ub", 0)
+    scores(0, 0)
+    tts(V("sel", 2, 4), V("lst", 0, 2), 0.0, A.add)
+    scores(0, 1)
+    ttt(V("sb"), by(V("tbm"), V("p8")), V("p4"), A.add)
+    run(calls[2:] + fours("kli"))
+    for b in (0, 10):
+        v = V("sb", 16 * AT[b] + 4, 16 * AT[b] + 8)
+        tts(v, v, col(8), A.add)
+    act(V("w0", T0 + N1, T0 + N1 + NF), V("yrow", 0, NF), ACT.Identity, scale=col(2), bias=col(6))
+    act(V("bs0"), V("sb", 0, NL + NF), ACT.Identity, bias=col(1))
+    for b, s, n in RUNS:
+        tts(V("rowc", 16 + b, 16 + b + s * (n - 1) + 1, s), V("yrow", 0, n), float(AT[b] + (CH // 16 - 8) * (AT[b] >= 8)), A.add)
+    tts(CW, V("yrow", 0, 16), 16.0, A.mult, col(9), A.add)
 
-    quant("uq", "us", 0, 128, "ub", 0, 512)
-    for i in range(2):
-        qstate(0, i)
-        score(0, i)
-    own_places()
-    for i in range(2):
-        find(i)
-        sign(i)
+    def partner_list(r):
+        return [lambda: act(V("kr"), by(V("ym"), V("rk%d" % r))), lambda: act(V("kk"), by(V("kr"), V("kof%d" % r)))] + [
+            lambda h=h: act(V("kd", 16 + 192 * h, 16 + 192 * h + HALF), V("kk", h, C, 2)) for h in range(2)]
 
     def register(r):
-        kof = "kof%d" % r
-        H1 = G0 + HALF
-        ttt(T.w0[:, G0:H1], T.bits[:, 0:C].indirect(T[kof][:, 0:10]), T.k1[:], A.add,
-            [("bits", 0, C), (kof, 0, 10), ("k1", 0, HALF)], [("w0", G0, H1)])
+        xt = "xt%d" % r
 
         def half(t):
-            act(T["yp%d" % r][:, C * t:C * t + C], T["xt%d" % r][:, 0:4 * C].indirect(T["k4%d" % r][:, 32 * t:32 * t + 20]), ACT.Copy,
-                [("xt%d" % r, 0, 4 * C), ("k4%d" % r, 32 * t, 32 * t + 20)], [("yp%d" % r, C * t, C * t + C)], scale=0.5)
+            act(V("yp", C * t, C * t + C), by(V(xt), V("k4", 32 * t, 32 * t + 20)), scale=0.5)
 
         def again(t):
-            act(T["yi%d" % r][:, C * t:C * t + C], T["yp%d" % r][:, C * t:C * t + C], ACT.Copy,
-                [("yp%d" % r, C * t, C * t + C)], [("yi%d" % r, C * t, C * t + C)])
+            act(V("yi", C * t, C * t + C), V("yp", C * t, C * t + C))
 
-        def blanks(i):
-            if r == 0:
-                blank("gg", 352 * i + 704, 352 * i + 720)
-                blank("gg", 352 * i + 1040, 352 * i + 1056)
-                blank("krs", C * i, C * i + C)
-        half(0)
-        half(1)
-        aside = [lambda: half(2), lambda: (half(3), again(0)), lambda: (again(1), again(2), blanks(0)),
-                 lambda: (again(3), blanks(1)), lambda: blanks(2)]
-        gap = find if r == 0 else (lambda i: None)
-        gap(2)
-        ttt(T.w0[:, H1:G0 + C], T.k3[:], T.w0[:, G0:H1], A.subtract, [("k3", 0, HALF), ("w0", G0, H1)], [("w0", H1, G0 + C)])
-        gap(3)
-        turn("w0", G0 - 16, HALF, None, lambda: gap(4))
-        gap(5)
-        wrapped("of0", 0, 1, 2, 1.0, float(LESS))
-        wrapped("ofs", 0, 1, 4, 1.0, float(LESS))
-        op("v", lambda e: e.tensor_copy(T.fi[:], TT.indirect(T.sel[:, 0:1])), [TN, SE], [("fi", 0, 16)])
-        cur, nxt = 352, 0
-        ttt(T.gg[:, 16:16 + NL], T.w0[:, 0:G0 + C].indirect(T.of0[:, 0:NB]), T.bs0[:], A.min,
-            [("w0", 0, G0 + C), ("of0", 0, 16), ("bs0", 0, NL)], [("gg", 16, 16 + NL)])
-        cur, nxt = nxt, cur
-        tts(T.fa[:], T.fi[:], 1, None, A.bitwise_and, None, [("fi", 0, 16)], [("fa", 0, 16)])
+        def level(at, n, off):
+            to = T0 + N1 + NF + at
+            ttt(V("w0", to, to + n), by(V("w0", T0, to), off), V("bs0", at, at + n), A.min)
+
+        def both(t, a, lo, hi, c):
+            o = C * t
+            ttt(V("zc", o + lo + a, o + hi, 2), V("yp", o + lo + a, o + hi, 2), V("yp", o + c, o + c + (hi - lo) // 2), A.add)
+
+        def beside(calls, small):
+            return [lambda c=c, s=small[i:i + 1]: (c(), run(s)) for i, c in enumerate(calls)]
+
+        def group(calls, n):
+            return [lambda c=c: run(calls[c:c + n]) for c in range(0, len(calls), n)]
+        for a, b in ((0, HALF), (HALF, C)):
+            ttt(V("w0", 16 + a, 16 + b), by(V("bits"), V("kpi", a // 16, b // 16)), V("sb", a, b), A.add)
+        for t in range(4):
+            half(t)
+        sums = [lambda t=t, a=a: both(t, a, 0, 192, HALF) for t in range(4) for a in range(2)]
+        few = [lambda t=t, a=a: both(t, a, CROSS, C, 128) for t in range(4) for a in range(2)]
+
+        def flags():
+            op("v", lambda e: e.tensor_copy(T.fi[:], T.ta[:, 0:2 * CH].indirect(T.sel[:, 4:5])), V("fi"), V("ta"), V("sel", 4, 5))
+        later.extend(second if r == 0 else [list, list] + sums[:2] + [lambda: (flags(), run(few[:2]))])
+        run(flips("ta", 0, "w0", 16, 128))
+        more = flips("ta", CH, "w0", 16 + 128, 192)
+        more[0]()
+        drip()
+        wrapped(V("ofa"), "ta", 0, 0.5, float(MID))
+        more[1]()
+        drip()
+        level(0, 64, V("ofa", 0, 4))
+        wrapped(V("ofb"), "ta", CH, 0.5, float(MID))
+        wrapped(V("ofl"), "ta", CH, 0.5, float(MID - N1))
+        level(64, 32, V("ofa", 4, 6))
+        tts(V("ofc"), V("ofb", 0, 2), float(N1 + NF + 127), A.min)
+        drip()
+        level(96, 32, V("ofa", 6, 8))
+        drip()
+        level(128, 32, V("ofc"))
+        drip()
+        ttt(V("gg", F0 - 16, F0 + NF), by(V("w0", T0, T0 + 336), V("ofb", 0, 8)), V("bs0", 128, 256), A.min)
+        signed = [
+            flags, lambda: run(flips("ta", 0, "w0", T0 + N1 + NF, NL)),
+            lambda: (tts(V("fa"), V("fi"), 1, A.arith_shift_right, 1, A.bitwise_and), wrapped(V("ofn"), "ta", 0, 0.5, float(MID - N1))),
+            lambda: (ttt(V("dat", 2, 96, 6), V("fa"), V("c2"), A.add), tts(V("dl", 2, 96, 6), V("fa"), -2.0, A.mult, 1.0, A.add))]
+        tail = [
+            lambda: run(flips("ta", 0, "kd", 16, HALF)), lambda: run(flips("ta", CH, "kd", 16 + 192, HALF)),
+            lambda: wrapped(V("eo"), "ta", 0, 1.0, 0.0, 2),
+            lambda: (ttt(V("dl", 4, 96, 6), V("eo", 16, 32), V("eo", 0, 16), A.subtract),
+                     ttt(V("dat", 5, 96, 6), V("eo", 16, 32), V("eo", 0, 16), A.add)),
+            lambda: ttt(V("ed"), V("dl", 4, 96, 6), V("c2"), A.mult),
+            lambda: ttt(V("dat", 4, 96, 6), V("eo", 0, 16), V("ed"), A.subtract)]
+        aside = [lambda: again(0), lambda: again(1), lambda: again(2), lambda: again(3)]
+        if r == 0:
+            pl = partner_list(0)
+            aside = [lambda: run(pl[:2]), lambda: (run(pl[2:]), again(0)), lambda: (again(1), again(2)), lambda: again(3)]
+            later.extend(group(rest[:3], 3) + signed + group(rest[3:], 2) + tail)
+        else:
+            small = signed[1:3] + beside(signed[3:], few[2:]) + tail[:2] + beside(tail[2:], few[3:]) + few[7:]
+            for i in range(6):
+                later.extend(sums[2 + i:3 + i] + small[2 * i:2 * i + 2])
+        cur, nxt = F0, G + F0
         for i, rad in enumerate(RADIX):
-            base, of = "bs%d" % (1 + i % 2), "of%d" % ((i + 1) % 2)
-            act(T[base][:], T.gg[:, cur + 16:cur + 16 + NL], ACT.Identity, [("gg", cur + 16, cur + 16 + NL)] + cc(1), [(base, 0, NL)], bias=col(1))
+            base, of = V("bs%d" % (1 + i % 2)), "of%d" % (i % 2)
+            drip()
+            act(base, V("gg", cur, cur + NF), ACT.Identity, bias=col(1))
             aside[i]()
-            flip(0, "gg", cur + 16, WIDE)
-            flip(WIDE, "gg", cur, WIDE)
-            if i == 0:
-                tts(T.dl[:, 2:64:4], T.fa[:], -2.0, 1.0, A.mult, A.add, [("fa", 0, 16)], [("dl", 0, 64)])
-            drip(1)
-            wrapped(of, 0, 1, 6, 1.0, float(LESS))
+            run(flips("tb", 0, "gg", cur, NF))
+            drip()
+            wrapped(V(of), "tb", 0, 0.5, float(MID - N1))
             for j in range(rad - 1):
-                if i == 2 and j == 0:
-                    ttt(T.dat[:, 2:64:4], T.fa[:], T.c2[:], A.add, [("fa", 0, 16), ("c2", 0, 16)], [("dat", 0, 64)])
-                else:
-                    drip(1)
-                ttt(T.gg[:, nxt + 16:nxt + 16 + NL], T.gg[:, cur + 16:cur + 16 + NL].indirect(T[of][:, 0:NB]), T[base][:], A.min,
-                    [("gg", cur + 16, cur + 16 + NL), (of, 0, 16), (base, 0, NL)], [("gg", nxt + 16, nxt + 16 + NL)])
+                drip()
+                ttt(V("gg", nxt, nxt + NF), by(V("gg", cur, cur + NF), V(of, 0, NF // 16)), base, A.min)
                 cur, nxt = nxt, cur
-        turn("gg", cur, 192, lambda: op("v", lambda e: e.tensor_copy(T.gg[:, cur + 16 + NL:cur + 336], T.gg[:, cur + 16:cur + 16 + NL].indirect(T.ofs[:, 0:NS // 16])),
-                                        [("gg", cur + 16, cur + 16 + NL), ("ofs", 0, 16)], [("gg", cur + 16 + NL, cur + 336)]))
-        drip(len(later))
-        for c, ct, sl in ((10, "ct1", 0), (8, "ct0", 1)):
-            ttt(T.dat[:, sl:64:4], TT.indirect(T.sel[:, c:c + 1]), T[ct][:], A.is_equal, [TN, SE, (ct, 0, 16)], [("dat", 0, 64)])
-        op("v", lambda e: e.tensor_tensor_scan(T.sc[:], T.dl[:], T.dat[:], 0.0, A.mult, A.add), [("dl", 0, 64), ("dat", 0, 64)], [("sc", 0, 64)])
-        tof = "tof%d" % r
-        for h in range(2):
-            tts(T[tof][:, 10 * h:10 * h + 10], T.sc[:, 2 + h:39 + h:4], 160.0, None, A.add, None, [("sc", 0, 64)], [(tof, 10 * h, 10 * h + 10)])
+        keepback = later[-1:]
+        drip(len(later) - 1)
+        later[:] = []
+        low = V("gg", cur, cur + NF)
+        act(V("gg", cur + NF, cur + NF + N1), by(low, V("ofl", 8, 12)))
+        tts(V("gg", cur - NL, cur), by(low, V("ofn", 0, NL // 16)), 0.0, A.add)
+        run(keepback)
+        run(flips("ta", 0, "gg", cur - NL, 128) + flips("ta", CH, "gg", cur - 16, 192))
+        for c, ct, sl in ((8, "ct1", 0), (6, "ct0", 1)):
+            ttt(V("dat", sl, 96, 6), by(V("ta"), V("sel", c, c + 1)), V(ct), A.is_equal)
+        op("v", lambda e: e.tensor_tensor_scan(T.sc[:, 0:60], T.dl[:, 0:60], T.dat[:, 0:60], 0.0, A.mult, A.add),
+           V("sc", 0, 60), V("dl", 0, 60), V("dat", 0, 60))
 
-    def pairs(r, a, b, some):
+    def pairs(a, b, some):
         for t in some:
-            yp, yi, tof = "yp%d" % r, "yi%d" % r, "tof%d" % r
-            ttt(T["zt%d" % r][:, 4 * a + t:4 * b:4], T[yp][:, C * t:C * t + C].indirect(T[tof][:, a // 16:b // 16]),
-                T[yi][:, C * t + a:C * t + b], A.add, [(yp, C * t, C * t + C), (yi, C * t + a, C * t + b), (tof, a // 16, b // 16)], [("zt%d" % r, 4 * a, 4 * b)])
+            ttt(V("zt", 4 * a + t, 4 * b, 4), by(V("yp", C * t, C * t + C), V("tof", a // 16, b // 16)), V("yi", C * t + a, C * t + b), A.add)
 
-    def layer(r, zcol, bk):
-        for b in range(4):
-            mul(bk + b, 128, "wq", "wp", 128 * b, "zq%d" % r, "zs%d" % r, zcol, zcol + 128)
+    def layer(zcol, n, bk, some):
+        for b in some:
+            mul(bk + b, "wq", "wp", 128 * b, "zq", "zs", zcol, zcol + n)
 
-    def keep(r, a, bk):
-        for b in range(4):
-            act(T["ht%d" % r][:, 4 * a + b:4 * a + 512:4], T.ps[:, 512 * (bk + b):512 * (bk + b) + 128], ACT.Copy,
-                [bank(bk + b)], [("ht%d" % r, 4 * a, 4 * a + 512)], scale=0.03125)
+    def keep(q, out, src):
+        if q == "a":
+            act(out, src, scale=0.03125)
+        else:
+            tts(out, src, 0.03125, A.mult)
+
+    def lay(r, i, t, q):
+        a, b = PARTS[i]
+        out, src = V("ht", 4 * a + t, 4 * b, 4), by(V("hp", HP * t, HP * t + CROSS + 16), V("rn%d" % r, a // 16, b // 16))
+        if q == "a":
+            act(out, src)
+        else:
+            tts(out, src, 0.0, A.add)
 
     def ship(r, i):
-        a = 128 * i
-        quant("hq%d" % r, "hs%d" % r, a, a + 128, "ht%d" % r, 4 * a, 4 * a + 512)
+        a, b = PARTS[i]
+        quant("hq%d" % r, "hs%d" % r, a, b, "ht", a)
         sem = "ar%d%d" % (i, r)
-        send(peer[r], T["rq%d" % r][:, a:a + 128].bitcast(dt.uint8), T["hq%d" % r][:, a:a + 128].bitcast(dt.uint8), [("hq%d" % r, a, a + 128)], sem)
-        send(peer[r], T["rs%d" % r][:, a:a + 128], T["hs%d" % r][:, a:a + 128], [("hs%d" % r, a, a + 128)], sem)
+        send(peer[r], raw(V("rq%d" % r, a, b)), raw(V("hq%d" % r, a, b)), sem)
+        send(peer[r], V("rs%d" % r, a, b), V("hs%d" % r, a, b), sem)
+        landed(sem, V("rq%d" % r, a, b), V("rs%d" % r, a, b))
 
-    def unpack(r, i, bk):
-        a = 128 * i
-        sem = "ar%d%d" % (i, r)
-        note("net", [], [("rq%d" % r, a, a + 128), ("rs%d" % r, a, a + 128)], sem, total[sem])
-        for b in range(4):
-            mul(bk + b, 128, "eq", "ep", 128 * b, "rq%d" % r, "rs%d" % r, a, a + 128)
-        for b in range(4):
-            act(T["bp%d" % r][:, C * b + a:C * b + a + 128], T.ps[:, 512 * (bk + b):512 * (bk + b) + 128], ACT.Copy,
-                [bank(bk + b)], [("bp%d" % r, C * b + a, C * b + a + 128)])
+    def unpack(r, i):
+        a, b = PARTS[i]
+        for t in range(4):
+            mul(4 * i + t, "eq", "ep", 128 * t, "rq%d" % r, "rs%d" % r, a, b)
+
+    def home(r, i):
+        a, b = PARTS[i]
+        for t in range(4):
+            ttt(V("xp", 4 * a + t, 4 * b, 4), by(V("hp", HP * t + CROSS, HP * t + HP), V("own", a // 16, b // 16)), V("xt%d" % r, 4 * a + t, 4 * b, 4), A.add)
 
     def advance(r, i, some):
         a, b = PARTS[i]
         for t in some:
-            bp, kof = "bp%d" % r, "kof%d" % (r + 1)
-            ttt(T["xt%d" % (r + 1)][:, 4 * a + t:4 * b:4], T[bp][:, C * t:C * t + C].indirect(T[kof][:, a // 16:b // 16]),
-                T["xt%d" % r][:, 4 * a + t:4 * b:4], A.add,
-                [(bp, C * t, C * t + C), (kof, a // 16, b // 16), ("xt%d" % r, 4 * a, 4 * b)], [("xt%d" % (r + 1), 4 * a, 4 * b)])
+            ttt(V("xt%d" % (r + 1), 4 * a + t, 4 * b, 4), bank(4 * i + t, 0, b - a), V("xp", 4 * a + t, 4 * b, 4), A.add)
 
     for r in range(ROUNDS):
         register(r)
-        if r == 0:
-            fetch(0)
-        nr = 352 * (2 + r)
-        kr, kk, kof, tof = C * r, "kk%d" % r, "kof%d" % r, "tof%d" % r
-        act(T[kk][:], T.krs[:, kr:kr + C].indirect(T[kof][:, 0:20]), ACT.Copy, [("krs", kr, kr + C), (kof, 0, 20)], [(kk, 0, C)])
-        act(T.gg[:, nr + 16:nr + 336], T[kk][:, 0:C].indirect(T[tof][:, 0:20]), ACT.Copy, [(kk, 0, C), (tof, 0, 20)], [("gg", nr + 16, nr + 336)])
-        zq, zs, zt = "zq%d" % r, "zs%d" % r, "zt%d" % r
-        pairs(r, 0, 128, range(4))
-        for i in range(2):
-            nxt = (128, 256) if i == 0 else (CROSS, C)
-            pairs(r, nxt[0], nxt[1], [0])
-            quant(zq, zs, 128 * i, 128 * i + 128, zt, 512 * i, 512 * i + 512)
-            layer(r, 128 * i, 4 * i)
-            keep(r, 128 * i, 4 * i)
-            pairs(r, nxt[0], nxt[1], [1, 2, 3] if i == 0 else [1, 2])
-        ship(r, 0)
-        pairs(r, CROSS, C, [3])
-        ship(r, 1)
-        quant(zq, zs, 256, 384, zt, 4 * 192, 4 * C)
-        layer(r, 256, 0)
-        for b in range(4):
-            act(T["bp%d" % r][:, C * b + CROSS:C * b + C], T.ps[:, 512 * b + 64:512 * b + 128], ACT.Copy,
-                [bank(b)], [("bp%d" % r, C * b + CROSS, C * b + C)], scale=0.03125)
-        turn("gg", nr, HALF)
-        wrapped("kof%d" % (r + 1), 0, 2, 0, 1.0, 160.0)
-        if r + 1 < ROUNDS:
-            k4 = "k4%d" % (r + 1)
-            for t in range(4):
-                wrapped(k4, 32 * t, 2, 0, 4.0, 640.0 + t)
-            dma("s", "dk%d" % (r + 1), [(T["lk%d" % (r + 1)][:, :], T.gg[0:128:16, nr + 16:nr + 336],
-                                         [("gg", nr + 16, nr + 336)], [("lk%d" % (r + 1), 0, 160)])])
-            share(r + 1)
-            fetch(r + 1)
-        else:
-            tts(T.kpf[:], T.gg[:, nr + 16:nr + 336], 160.0, None, A.add, None, [("gg", nr + 16, nr + 336)], [("kpf", 0, C)])
-            dma("s", "okp", [(T.kp[:, :], T.kpf[0:128:16, :], [("kpf", 0, C)], [])])
-            quant("vq", "vs", 0, 128, "vb", 0, 512)
-        if r == 0:
-            quant("eq", "ep", 0, 512, "eb", 0, 2048)
-        unpack(r, 0, 4)
-        unpack(r, 1, 0)
-        n = r + 1
-        advance(r, 0, range(4))
-        advance(r, 1, [0])
+        n, kof = r + 1, "kof%d" % (r + 1)
+        nm = "nm%d" % r
+        for h in range(2):
+            tts(V(nm, 10 * h, 10 * h + 10), V("sc", 5 - h, 60, 6), 160.0, A.add, float(CROSS), A.min)
+        send(peer[r], V("rn%d" % r), V(nm), "arn%d" % r)
+        landed("arn%d" % r, V("rn%d" % r))
+        for h in range(2):
+            tts(V("tof", 10 * h, 10 * h + 10), V("sc", 2 + h, 60, 6), 160.0, A.add)
+        for h in range(2):
+            tts(V(kof, 10 * h, 10 * h + 10), V("sc", 5 - h, 60, 6), 160.0, A.add)
         if n < ROUNDS:
-            qstate(n, 0)
-            score(n, 0)
-            advance(r, 1, [1, 2, 3])
-            qstate(n, 1)
-            score(n, 1)
-            sign(0)
-            sign(1)
+            share(n)
+        if r == 0:
+            pairs(0, CROSS, range(4))
+        else:
+            for t in range(4):
+                act(V("zt", 512 + t, 1024, 4), by(V("zc", C * t, C * t + C), V("tof", 8, 16)))
+            pairs(0, 128, range(4))
+        pairs(CROSS, C, [0])
+        quant("zq", "zs", 0, CROSS, "zt", 0)
+        layer(0, CROSS, 0, [0, 2, 1, 3])
+        pairs(CROSS, C, [1, 2, 3])
+        for t, q in ((0, "a"), (2, "v"), (1, "a"), (3, "v")):
+            keep(q, V("hp", HP * t, HP * t + CROSS), bank(t, 0, CROSS))
+            if t == 2:
+                quant("zq", "zs", 256, 384, "zt", 192)
+                layer(256, 128, 4, range(4))
+        tts(V("own"), V(kof), float(16 - CROSS), A.add)
+        for t, q in ((0, "a"), (2, "v"), (1, "a"), (3, "v")):
+            lay(r, 0, t, q)
+        lay(r, 1, 0, "a")
+        lay(r, 1, 1, "a")
+        ship(r, 0)
+        lay(r, 1, 2, "v")
+        lay(r, 1, 3, "v")
+        lists = scores_list(kof) + fours(kof) if n < ROUNDS else []
+        run(lists[:2])
+        ship(r, 1)
+        for t in range(4):
+            keep("a", V("hp", HP * t + CROSS + 16, HP * t + HP), bank(4 + t, 64, 128))
+        if n < ROUNDS:
+            run(lists[2:] + partner_list(n))
+        else:
+            act(V("kpf"), by(V("yrow"), V(kof)))
+            dma("s", "okp", [(T.kp[:, :], (T.kpf[0:128:16, :], V("kpf")[1]))])
+            quant("vq", "vs", 0, 128, "vb", 0)
+        if r == 0:
+            quant("eq", "ep", 0, 512, "eb", 0)
+        home(r, 0)
+        unpack(r, 0)
+        home(r, 1)
+        unpack(r, 1)
+        advance(r, 0, range(4))
+        if n < ROUNDS:
+            scores(n, 0)
+            advance(r, 1, range(4))
+            scores(n, 1)
         else:
             for i in range(2):
                 a, b = PARTS[i]
                 if i == 1:
-                    advance(r, 1, [1, 2, 3])
-                qstate(n, i)
-                mul(4 + i, b - a, "vq", "vs", 0, "xq%d" % n, "xs%d" % n, a, b)
-                act(T.yo[:, a:b], T.ps[:, 512 * (4 + i):512 * (4 + i) + b - a], ACT.Copy, [bank(4 + i)], [("yo", a, b)])
-                dma("s", "oc%d" % i, [(T.oc[:, 4 * a:4 * b], T["xq%d" % n][:, a:b].bitcast(dt.uint8), [("xq%d" % n, a, b)], [])])
-                dma("a", "oy%d" % i, [(T.y[:, a:b], T.yo[:, a:b], [("yo", a, b)], [])])
-            dma("s", "os", [(T.osc[4 * i:4 * i + 4, :], T["xs%d" % n][32 * i:32 * i + 4, :], [("xs%d" % n, 0, C)], []) for i in range(4)])
+                    advance(r, 1, range(4))
+                quant("xq", "xs", a, b, "xt%d" % n, a)
+                mul(i, "vq", "vs", 0, "xq", "xs", a, b)
+                act(V("yo", a, b), bank(i, 0, b - a))
+                dma("s", "oc%d" % i, [(T.oc[:, 4 * a:4 * b], raw(V("xq", a, b)))])
+                dma("a", "oy%d" % i, [(T.y[:, a:b], V("yo", a, b))])
+            dma("s", "os", [(T.osc[4 * i:4 * i + 4, :], (T.xs[32 * i:32 * i + 4, :], V("xs")[1])) for i in range(4)])
     for sem in total:
         if seen["g"].get(sem, 0) < total[sem]:
             g.wait_ge(T.sem[sem], total[sem])

@@ -15,7 +15,7 @@ T0 = 16 + NL + NF
 FAR, CH = 192, 416
 G, F0 = 352, 16 + NL
 PARTS = [(0, 192), (192, C)]
-HP = C + 16
+ZW = CROSS + C
 F32, BF, I32, U16, F8, U8 = "float32", "bfloat16", "int32", "uint16", "float8_e4m3fn_x4", "uint8"
 
 
@@ -29,7 +29,7 @@ def _sb(n, kind):
 
 SCRATCH = {
     "ub": _sb(512, BF), "vb": _sb(512, BF), "uq": _sb(128, F8), "us": _sb(128, U8), "vq": _sb(128, F8), "vs": _sb(128, U8),
-    "wq": _sb(512, F8), "wp": _sb(512, U8), "one": _sb(512, BF), "eb": _sb(2048, BF), "eq": _sb(512, F8), "ep": _sb(512, U8),
+    "wq": _sb(512, F8), "wp": _sb(512, U8), "one": _sb(516, BF), "eb": _sb(516, BF), "eq": _sb(512, F8), "ep": _sb(512, U8),
     "pidx": _sb(1, I32), "qidx": _sb(1, I32), "grp": _sb(1, I32), "par": _sb(1, I32), "q8": _sb(1, I32),
     "yrow": _sb(C, F32), "ym": _sb(C, BF), "cst": _sb(16, F32), "sel": _sb(12, U16), "rowc": _sb(112, BF), "lst": _sb(16, F32),
     "ki": _sb(2, I32), "kj": _sb(2, I32), "kf": _sb(2, F32), "tab": _sb(32, F32), "tbm": _sb(40, F32), "pu": _sb(20, U16), "p8": _sb(20, U16),
@@ -40,22 +40,23 @@ SCRATCH = {
     "eo": _sb(32, F32), "ed": _sb(16, F32), "kli": _sb(20, I32), "kw": _sb(32, F32), "kpi": _sb(32, U16), "k4": _sb(128, U16),
     "w0": _sb(T0 + 336, BF), "gg": _sb(2 * G, BF), "bits": _sb(2 * C, BF), "ta": _sb(2 * CH, BF), "tb": _sb(CH, BF),
     "ofa": _sb(16, U16), "ofb": _sb(16, U16), "ofc": _sb(2, U16), "ofl": _sb(16, U16), "ofn": _sb(16, U16), "of0": _sb(16, U16), "of1": _sb(16, U16),
-    "kr": _sb(C, BF), "kk": _sb(C, BF), "kd": _sb(400, BF), "tof": _sb(20, U16), "own": _sb(20, U16),
-    "yp": _sb(4 * C, BF), "yi": _sb(4 * C, BF), "zc": _sb(4 * C, BF), "zt": _sb(4 * C, BF), "zq": _sb(384, F8), "zs": _sb(384, U8),
-    "hp": _sb(4 * HP, BF), "ht": _sb(4 * C, BF), "xp": _sb(4 * C, BF),
+    "kr": _sb(C, BF), "kk": _sb(C, BF), "kd": _sb(400, BF), "tof": _sb(20, U16),
+    "yp": _sb(4 * C, BF), "yi": _sb(4 * C, BF), "zc": _sb(2 * ZW, BF), "zt": _sb(4 * C, BF), "zq": _sb(384, F8), "zs": _sb(384, U8),
+    "hw": _sb(4 * (C - CROSS), BF), "ht": _sb(4 * CROSS, BF), "xv": _sb(4 * C, BF),
+    "nv": _sb(G, BF), "nw": _sb(G, BF), "ki2": _sb(32, U16), "t1": _sb(C, BF), "i4": _sb(128, U16),
     "xq": _sb(C, F8), "xs": _sb(C, U8), "kpf": _sb(C, F32), "yo": _sb(C, F32),
     "ps": ("psum", [128, 4096], F32),
 }
 for _r in range(ROUNDS + 1):
     SCRATCH["xt%d" % _r] = _sb(4 * C, BF)
-    SCRATCH["kof%d" % _r] = _sb(20, U16)
+    SCRATCH["kof%d" % _r] = _sb(52, U16)
 for _r in range(ROUNDS):
-    for _n, _k, _w in (("hq", F8, C), ("hs", U8, C), ("rq", F8, C), ("rs", U8, C), ("nm", U16, 20), ("rn", U16, 20), ("rk", U16, 20)):
+    for _n, _k, _w in (("hq", F8, CROSS), ("hs", U8, CROSS), ("rq", F8, CROSS), ("rs", U8, CROSS), ("rk", U16, 40)):
         SCRATCH["%s%d" % (_n, _r)] = _sb(_w, _k)
 SEMAPHORES = ["sv", "sa", "sp", "sg", "sent", "lx0", "lx1", "lu", "lv", "lk", "lwc", "lws",
               "oc0", "oc1", "os", "oy0", "oy1", "okp"]
 for _r in range(ROUNDS):
-    SEMAPHORES += ["ark%d" % _r, "arn%d" % _r, "ar0%d" % _r, "ar1%d" % _r]
+    SEMAPHORES += ["ark%d" % _r, "ar0%d" % _r, "ar1%d" % _r]
 
 
 def rank_program(g, core, T, topo):
@@ -145,8 +146,8 @@ def rank_program(g, core, T, topo):
     def iota(out, pattern, base, mult, **k):
         op("g", lambda e: e.iota(out[0], pattern, base, mult, **k), out)
 
-    def quant(q, s, a, b, t, ta):
-        qv, sv, tv = V(q, a, b), V(s, a, b), V(t, 4 * ta, 4 * (ta + b - a))
+    def quant(q, s, a, b, t, ta, shift=0):
+        qv, sv, tv = V(q, a, b), V(s, a, b), V(t, 4 * ta + shift, 4 * (ta + b - a) + shift)
         op("v", lambda e: e.quantize_mx(qv[0], sv[0], tv[0]), (None, qv[1] + sv[1]), tv)
 
     def bank(i, a, b):
@@ -184,11 +185,12 @@ def rank_program(g, core, T, topo):
     peer = [T.cores[rank ^ m] for m in MASKS]
     dma("s", "lx0", [(V("xt0", 0, 768), T.x[:, 0:768])])
     dma("a", "lk", [(V("kli"), T.kl[:, :])])
-    dma("s", "lx1", [(V("xt0", 768, 1280), T.x[:, 768:1280])])
     dma("a", "lu", [(V("ub"), T.u[:, :])])
+    dma("s", "lx1", [(V("xt0", 768, 1280), T.x[:, 768:1280])])
+    need("s", V("xt0")[1] + V("ub")[1], [])
     dma("s", "lwc", [(raw(V("wq")), T.wc[:, 0:2048])])
     dma("s", "lws", [(V("wp"), T.ws[:, 0:512])])
-    dma("a", "lv", [(V("vb"), T.v[:, :])])
+    dma("s", "lv", [(V("vb"), T.v[:, :])])
 
     small = {"allow_small_or_imprecise_dtypes": True}
     Q, GR = V("qidx"), V("grp")
@@ -207,70 +209,69 @@ def rank_program(g, core, T, topo):
     tts(col(9), Q, 1.0, A.mult)
     tts(col(10), Q, 11.0, A.min, 16.0, A.mult)
     tts(col(11), V("q8"), 1.0, A.mult)
-    tts(V("par"), Q, col(5), A.add)
     tts(col(7), col(0), 3.0, A.mult, 1.0, A.add)
-    tts(V("par"), V("par"), 1, A.bitwise_and)
-    tts(col(1), col(0), BIG, A.mult)
-    tts(col(2), col(0), 2.0, A.mult)
-    tts(V("sel", 0, 1), V("par"), float(FAR + 16), A.mult, col(10), A.add)
+    tts(V("par"), Q, col(5), A.add)
 
     def blank(nm, a, b):
         for c in range(a, b, 512):
             act(V(nm, c, min(b, c + 512)), V("one", 0, min(b - c, 512)), scale=0.0)
     blank("tb", 0, CH)
-    blank("ta", 0, 2 * CH)
-    for b, s, n in RUNS:
-        tts(V("rowc", 64 + AT[b], 64 + AT[b] + n), V("yrow", 0, n), float(s), A.mult, float(b), A.add)
+    for i, (b, s, n) in enumerate(RUNS):
+        out = V("rowc", 64 + AT[b], 64 + AT[b] + n)
+        if i < 4:
+            act(out, V("yrow", b, b + s * (n - 1) + 1, s))
+        else:
+            tts(out, V("yrow", 0, n), float(s), A.mult, float(b), A.add)
+    tts(V("par"), V("par"), 1, A.bitwise_and)
+    tts(col(8), col(0), 32.0 * (20 - table_at(AT[0])), A.mult)
+    tts(col(2), col(0), 2.0, A.mult)
+    tts(col(6), col(0), 2.0 * (N1 - MID) - BIG, A.mult, BIG, A.add)
+    tts(V("sel", 0, 1), V("par"), float(FAR + 16), A.mult, col(10), A.add)
     tts(V("pu"), V("rowc", 64, 84), 16.0, A.mult, col(9), A.add)
     tts(V("p8"), V("rowc", 64, 84), 2.0, A.mult, col(11), A.add)
-    act(V("p4"), by(V("yrow"), V("pu")), ACT.Identity, scale=col(7))
-    blank("gg", F0 + NF, G + F0)
-    blank("gg", G + F0 + NF, 2 * G)
-    act(V("ym"), V("yrow"), ACT.Identity, bias=-160.0)
     blank("w0", 0, 16)
+    act(V("p4"), by(V("yrow"), V("pu")), ACT.Identity, scale=col(7))
+    for b in (0, 10):
+        v = V("p4", 16 * AT[b] + 4, 16 * AT[b] + 8)
+        act(v, v, ACT.Identity, bias=col(8))
     run(flips("tb", 0, "rowc", 64, 32))
     tts(col(3), col(0), -1.0, A.mult)
     tts(col(4), col(0), TINY, A.mult)
-    tts(col(12), col(0), -TINY, A.mult)
+    tts(col(1), col(0), BIG, A.mult)
     wrapped(V("lst"), "tb", 0, 1.0, 0.0)
-    tts(V("kof0"), V("kli"), 0.0, A.add)
-    tts(V("tbm", 0, 20), V("tab", 0, 20), 1.0, A.add, col(0), A.mult)
-    tts(V("tbm", 20, 40), V("tab", 0, 20), float(1 - 2 * C), A.add, col(0), A.mult)
-    tts(col(8), col(0), 32.0 * (20 - table_at(AT[0])), A.mult)
-    tts(col(6), col(0), 2.0 * (N1 - MID) - BIG, A.mult, BIG, A.add)
 
     def scores_list(k):
         return [lambda: tts(V("kw", 0, 10), V(k, 0, 10), 0.0, A.add), lambda: tts(V("kw", 10, 20), V(k, 0, 10), float(C), A.add),
                 lambda: tts(V("kpi"), by(V("kw"), V("sel", 2, 4)), 0.0, A.add)]
 
     def share(r):
-        send(peer[r], V("rk%d" % r), V("kof%d" % r), "ark%d" % r)
-        landed("ark%d" % r, V("rk%d" % r))
+        w = 40 if r else 20
+        send(peer[r], V("rk%d" % r, 0, w), V("kof%d" % r, 0, w), "ark%d" % r)
+        landed("ark%d" % r, V("rk%d" % r, 0, w))
 
-    share(0)
-    iota(V("kd"), [[0, 400]], 0, 0, **small)
-    for t in range(4):
-        iota(V("zc", C * t + 192, C * t + CROSS), [[0, 64]], 0, 0, **small)
-        iota(V("hp", HP * t + CROSS, HP * t + CROSS + 16), [[0, 16]], 0, 0, **small)
-    for b in range(4):
-        op("g", lambda e: e.affine_select(T.eb[:, 512 * b:512 * b + 512], T.one[:], [[1, 512]], A.is_equal, 0.0, -b, -4),
-           V("eb", 512 * b, 512 * b + 512), V("one"))
+    for b, s, n in RUNS:
+        iota(V("rowc", 16 + b, 16 + b + s * (n - 1) + 1, s), [[1, n]], AT[b] + (CH // 16 - 8) * (AT[b] >= 8), 0, **small)
+    blank("gg", F0 + NF, G + F0)
+    blank("gg", G + F0 + NF, 2 * G)
+    act(V("w0", T0 + N1, T0 + N1 + NF), V("yrow", 0, NF), ACT.Identity, scale=col(2), bias=col(6))
+    for a in (128, 352):
+        blank("ta", a, a + 64)
+    iota(V("dl"), [[0, 16], [-1, 2], [0, 3]], 0, 0, **small)
     LH = V("lst", 0, 4, 2)
     CW = V("cw")
     second = [
-        lambda: tts(V("rowc", 48, 64), V("rowc", 26, 42), 0.0, A.add),
         lambda: run(flips("tb", 0, "rowc", 16, 48)),
         lambda: wrapped(V("lst"), "tb", 0, 1.0, 0.0),
-        lambda: (tts(V("ki"), LH, col(5), A.add), tts(V("c2"), CW, 2.0, A.mult, -160.0, A.add)),
-        lambda: (tts(V("kj"), V("ki"), 1, A.bitwise_and), fill(V("dl"), -1.0)),
+        lambda: tts(V("ki"), LH, col(5), A.add),
+        lambda: tts(V("kj"), V("ki"), 1, A.bitwise_and),
         lambda: tts(V("kf"), V("kj"), float(FAR // 16 + 1), A.mult),
         lambda: ttt(V("kf"), V("kf"), LH, A.add)]
     rest = [
         lambda: tts(V("sel", 4, 5), V("kf", 0, 1), 16.0, A.mult),
         lambda: tts(V("sel", 6, 10, 2), V("kf"), 16.0, A.mult, 1.0, A.add),
         lambda: tts(V("sel", 1, 2), V("sel", 0, 1), float(CH), A.add),
+        lambda: tts(V("c2"), CW, 2.0, A.mult, -160.0, A.add),
         lambda: tts(V("dat", 3, 96, 6), CW, 4.0, A.mult, -319.0, A.add),
-        lambda: fill(V("dl", 0, 96, 6), 0.0),
         lambda: tts(V("ca"), CW, 0.0, A.is_equal),
         lambda: tts(V("ce"), CW, 159.0, A.is_equal, 2.0, A.mult),
         lambda: tts(V("cb"), CW, 159.0, A.is_equal, -160.0, A.mult),
@@ -279,36 +280,59 @@ def rank_program(g, core, T, topo):
         lambda: tts(V("cd"), CW, 159.0, A.is_equal, 161.0, A.mult),
         lambda: ttt(V("ct0"), V("ca"), V("cb"), A.add),
         lambda: ttt(V("ct1"), V("ca"), V("cd"), A.add)]
+    natural = [
+        lambda: (tts(col(14), V("par"), float(FAR + 16), A.mult), tts(col(13), Q, 3.0, A.min, 16.0, A.mult)),
+        lambda: (tts(col(12), col(11), float(CH - 128), A.mult, col(14), A.add),
+                 tts(V("sel", 11, 12), col(13), col(14), A.add, float(CH + 128), A.add)),
+        lambda: tts(V("sel", 10, 11), Q, 16.0, A.mult, col(12), A.add)]
 
-    def scores(r, i):
+    def scores(r, i, between=list):
         a, b = PARTS[i]
         quant("xq", "xs", a, b, "xt%d" % r, a)
-        mul(i, "uq", "us", 0, "xq", "xs", a, b)
-        act(V("bits", a, b), bank(i, 0, b - a), ACT.Sign, scale=col(0), bias=col(12))
-        act(V("bits", C + a, C + b), bank(i, 0, b - a), ACT.Sign, scale=col(3), bias=col(4))
+        between()
+        for j in range(1 + i):
+            mul(i + j, "uq", "us", 0, "xq", "xs", a, b)
+        if i:
+            act(V("bits", C + a, C + b), bank(i, 0, b - a), ACT.Sign, scale=col(3), bias=col(4))
+
+    def signs(between):
+        (a, b), (c, d) = PARTS
+        tts(V("bits", a, b), bank(0, 0, b - a), 0.0, A.is_gt, col(2), A.mult)
+        run(between)
+        tts(V("bits", C + a, C + b), V("bits", a, b), -1.0, A.mult, col(0), A.add)
+        tts(V("bits", c, d), bank(2, 0, d - c), 0.0, A.is_gt, col(2), A.mult)
 
     def fours(k):
-        return [lambda t=t: tts(V("k4", 32 * t, 32 * t + 20), V(k), 4.0, A.mult, float(t), A.add) for t in range(4)]
+        return [lambda t=t: tts(V("k4", 32 * t, 32 * t + 20), V(k, 0, 20), 4.0, A.mult, float(t), A.add) for t in range(4)]
 
     calls = scores_list("kli")
+    tts(V("kof0", 0, 20), V("kli"), 0.0, A.add)
     run(calls[:2])
-    quant("uq", "us", 0, 128, "ub", 0)
-    scores(0, 0)
     tts(V("sel", 2, 4), V("lst", 0, 2), 0.0, A.add)
-    scores(0, 1)
-    ttt(V("sb"), by(V("tbm"), V("p8")), V("p4"), A.add)
-    run(calls[2:] + fours("kli"))
-    for b in (0, 10):
-        v = V("sb", 16 * AT[b] + 4, 16 * AT[b] + 8)
-        tts(v, v, col(8), A.add)
-    act(V("w0", T0 + N1, T0 + N1 + NF), V("yrow", 0, NF), ACT.Identity, scale=col(2), bias=col(6))
-    act(V("bs0"), V("sb", 0, NL + NF), ACT.Identity, bias=col(1))
-    for b, s, n in RUNS:
-        tts(V("rowc", 16 + b, 16 + b + s * (n - 1) + 1, s), V("yrow", 0, n), float(AT[b] + (CH // 16 - 8) * (AT[b] >= 8)), A.add)
+    tts(V("tbm", 0, 20), V("tab", 0, 20), col(0), A.mult)
+    tts(V("tbm", 20, 40), V("tab", 0, 20), float(1 - 2 * C), A.add, col(0), A.mult)
     tts(CW, V("yrow", 0, 16), 16.0, A.mult, col(9), A.add)
+    run(calls[2:])
+    scores(0, 0, lambda: quant("uq", "us", 0, 128, "ub", 0))
+    for a in (0, HALF):
+        ttt(V("sb", a, a + HALF), by(V("tbm"), V("p8", a // 16, a // 16 + 10)), V("p4", a, a + HALF), A.add)
+        if a == 0:
+            scores(0, 1)
+    signs(fours("kli")[1:])
+    act(V("rowc", 48, 64), V("rowc", 26, 42))
+    act(V("bs0"), V("sb", 0, NL + NF), ACT.Identity, bias=col(1))
+    run(fours("kli")[:1])
+    share(0)
+    op("g", lambda e: e.affine_select(T.eb[:], T.one[:], [[1, 516]], A.is_equal, 0.0, -3, -4), V("eb"), V("one"))
+    for t in range(2):
+        iota(V("zc", ZW * t + CROSS + 192, ZW * t + 2 * CROSS), [[0, 64]], 0, 0, **small)
+    iota(V("nv"), [[0, G]], 0, 0, **small)
+    for a in (0, G - 16):
+        iota(V("nw", a, a + 16), [[0, 16]], 0, 0, **small)
+    iota(V("t1"), [[1, HALF], [HALF, 2]], -HALF, 0, **small)
 
     def partner_list(r):
-        return [lambda: act(V("kr"), by(V("ym"), V("rk%d" % r))), lambda: act(V("kk"), by(V("kr"), V("kof%d" % r)))] + [
+        return [lambda: act(V("kr"), by(V("ym"), V("rk%d" % r, 0, 20))), lambda: act(V("kk"), by(V("kr"), V("kof%d" % r, 0, 20)))] + [
             lambda h=h: act(V("kd", 16 + 192 * h, 16 + 192 * h + HALF), V("kk", h, C, 2)) for h in range(2)]
 
     def register(r):
@@ -317,16 +341,16 @@ def rank_program(g, core, T, topo):
         def half(t):
             act(V("yp", C * t, C * t + C), by(V(xt), V("k4", 32 * t, 32 * t + 20)), scale=0.5)
 
-        def again(t):
-            act(V("yi", C * t, C * t + C), V("yp", C * t, C * t + C))
+        def again(t, a):
+            act(V("yi", C * t + a, C * t + C), V("yp", C * t + a, C * t + C))
 
         def level(at, n, off):
             to = T0 + N1 + NF + at
             ttt(V("w0", to, to + n), by(V("w0", T0, to), off), V("bs0", at, at + n), A.min)
 
-        def both(t, a, lo, hi, c):
-            o = C * t
-            ttt(V("zc", o + lo + a, o + hi, 2), V("yp", o + lo + a, o + hi, 2), V("yp", o + c, o + c + (hi - lo) // 2), A.add)
+        def both(t, a, at, lo, hi, c):
+            o, z = C * t, ZW * (t - 2) + at
+            ttt(V("zc", z + lo + a, z + hi, 2), V("yp", o + lo + a, o + hi, 2), V("yp", o + c, o + c + (hi - lo) // 2), A.add)
 
         def beside(calls, small):
             return [lambda c=c, s=small[i:i + 1]: (c(), run(s)) for i, c in enumerate(calls)]
@@ -335,14 +359,14 @@ def rank_program(g, core, T, topo):
             return [lambda c=c: run(calls[c:c + n]) for c in range(0, len(calls), n)]
         for a, b in ((0, HALF), (HALF, C)):
             ttt(V("w0", 16 + a, 16 + b), by(V("bits"), V("kpi", a // 16, b // 16)), V("sb", a, b), A.add)
-        for t in range(4):
+        for t in (2, 3, 0, 1):
             half(t)
-        sums = [lambda t=t, a=a: both(t, a, 0, 192, HALF) for t in range(4) for a in range(2)]
-        few = [lambda t=t, a=a: both(t, a, CROSS, C, 128) for t in range(4) for a in range(2)]
+        sums = [lambda t=t, a=a, w=w: both(t, a, *w) for t in (2, 3) for w in ((CROSS, 0, 192, HALF), (0, 0, CROSS, 0)) for a in range(2)]
+        few = [lambda t=t, a=a: both(t, a, CROSS, CROSS, C, 128) for t in (2, 3) for a in range(2)] + [list] * 4
 
         def flags():
             op("v", lambda e: e.tensor_copy(T.fi[:], T.ta[:, 0:2 * CH].indirect(T.sel[:, 4:5])), V("fi"), V("ta"), V("sel", 4, 5))
-        later.extend(second if r == 0 else [list, list] + sums[:2] + [lambda: (flags(), run(few[:2]))])
+        later.extend(beside(second, [list, rest[5]] + group(rest[6:8], 2) + group([rest[8], rest[3], rest[9], rest[4]], 2) + natural[:1]) if r == 0 else [list, list] + sums[:2] + [lambda: (flags(), run(few[:2]))])
         run(flips("ta", 0, "w0", 16, 128))
         more = flips("ta", CH, "w0", 16 + 128, 192)
         more[0]()
@@ -372,15 +396,24 @@ def rank_program(g, core, T, topo):
                      ttt(V("dat", 5, 96, 6), V("eo", 16, 32), V("eo", 0, 16), A.add)),
             lambda: ttt(V("ed"), V("dl", 4, 96, 6), V("c2"), A.mult),
             lambda: ttt(V("dat", 4, 96, 6), V("eo", 0, 16), V("ed"), A.subtract)]
-        aside = [lambda: again(0), lambda: again(1), lambda: again(2), lambda: again(3)]
+        pl = partner_list(r)
+        aside = [lambda: run(pl[:2]), lambda: (run(pl[2:]), again(0, 0)), lambda: (again(1, 0), again(2, CROSS)), lambda: again(3, CROSS)]
         if r == 0:
-            pl = partner_list(0)
-            aside = [lambda: run(pl[:2]), lambda: (run(pl[2:]), again(0)), lambda: (again(1), again(2)), lambda: again(3)]
-            later.extend(group(rest[:3], 3) + signed + group(rest[3:], 2) + tail)
+            act(V("ym"), V("yrow"), ACT.Identity, bias=-160.0)
+            aside = [lambda: (again(0, 0), again(1, 0), blank("kd", 0, 400)), aside[0], lambda: (run(pl[2:]), again(2, CROSS)), aside[3]]
+            small = group(rest[:3], 3) + beside(signed, group([rest[10], few[0]], 2) + rest[11:] + few[1:]) + tail[:2] + beside(tail[2:4], few[2:])
+            sums[:2] = beside(sums[:2], natural[1:])
+            for i in range(5):
+                later.extend(small[i:i + 1] + sums[i:i + 1])
+            later.extend(sums[5:6] + small[5:7] + sums[6:7] + small[7:8] + sums[7:] + small[8:])
         else:
-            small = signed[1:3] + beside(signed[3:], few[2:]) + tail[:2] + beside(tail[2:], few[3:]) + few[7:]
-            for i in range(6):
-                later.extend(sums[2 + i:3 + i] + small[2 * i:2 * i + 2])
+            aside[2] = lambda: (act(V("nw", 16, 16 + C), by(V("nv", 16, 16 + C), V("rk%d" % r, 20, 40))), again(1, 0))
+            aside[3] = lambda: (again(2, CROSS), again(3, CROSS))
+            through = [lambda: run(flips("ta", 0, "nw", 16, 128)), lambda: run(flips("ta", CH, "nw", 16 + 128, 192)),
+                       lambda: tts(V("ki2"), by(V("ta"), V("sel", 10, 12)), 160.0, A.add)]
+            later.extend(sums[2:3] + signed[1:3] + sums[3:4] + beside(signed[3:], few[2:]) + sums[4:6] + few[3:4] + sums[6:7]
+                         + tail[:2] + sums[7:] + tail[2:4] + through + tail[4:] + [list])
+            later.append((lambda: quant("vq", "vs", 0, 128, "vb", 0)) if r == 1 else list)
         cur, nxt = F0, G + F0
         for i, rad in enumerate(RADIX):
             base, of = V("bs%d" % (1 + i % 2)), "of%d" % (i % 2)
@@ -394,18 +427,21 @@ def rank_program(g, core, T, topo):
                 drip()
                 ttt(V("gg", nxt, nxt + NF), by(V("gg", cur, cur + NF), V(of, 0, NF // 16)), base, A.min)
                 cur, nxt = nxt, cur
-        keepback = later[-1:]
-        drip(len(later) - 1)
-        later[:] = []
+        if r == 0:
+            later.extend(beside(tail[4:] + [list, list], [lambda b=b: quant("eq", "ep", 128 * b, 128 * b + 128, "eb", 0, 3 - b) for b in range(4)]))
+        drip(max(len(later) - 4, 1))
         low = V("gg", cur, cur + NF)
         act(V("gg", cur + NF, cur + NF + N1), by(low, V("ofl", 8, 12)))
         tts(V("gg", cur - NL, cur), by(low, V("ofn", 0, NL // 16)), 0.0, A.add)
-        run(keepback)
+        drip()
         run(flips("ta", 0, "gg", cur - NL, 128) + flips("ta", CH, "gg", cur - 16, 192))
+        drip()
         for c, ct, sl in ((8, "ct1", 0), (6, "ct0", 1)):
             ttt(V("dat", sl, 96, 6), by(V("ta"), V("sel", c, c + 1)), V(ct), A.is_equal)
+        drip()
         op("v", lambda e: e.tensor_tensor_scan(T.sc[:, 0:60], T.dl[:, 0:60], T.dat[:, 0:60], 0.0, A.mult, A.add),
            V("sc", 0, 60), V("dl", 0, 60), V("dat", 0, 60))
+        drip(len(later))
 
     def pairs(a, b, some):
         for t in some:
@@ -421,107 +457,125 @@ def rank_program(g, core, T, topo):
         else:
             tts(out, src, 0.03125, A.mult)
 
-    def lay(r, i, t, q):
-        a, b = PARTS[i]
-        out, src = V("ht", 4 * a + t, 4 * b, 4), by(V("hp", HP * t, HP * t + CROSS + 16), V("rn%d" % r, a // 16, b // 16))
+    def pick(q, out, src):
         if q == "a":
             act(out, src)
         else:
             tts(out, src, 0.0, A.add)
 
     def ship(r, i):
-        a, b = PARTS[i]
+        a, b = 128 * i, 128 * i + 128
         quant("hq%d" % r, "hs%d" % r, a, b, "ht", a)
-        sem = "ar%d%d" % (i, r)
-        send(peer[r], raw(V("rq%d" % r, a, b)), raw(V("hq%d" % r, a, b)), sem)
-        send(peer[r], V("rs%d" % r, a, b), V("hs%d" % r, a, b), sem)
-        landed(sem, V("rq%d" % r, a, b), V("rs%d" % r, a, b))
+        if i:
+            send(peer[r], V("rs%d" % r), V("hs%d" % r), "ar0%d" % r)
+            landed("ar0%d" % r, V("rq%d" % r, 0, 128), V("rs%d" % r))
+        send(peer[r], raw(V("rq%d" % r, a, b)), raw(V("hq%d" % r, a, b)), "ar%d%d" % (i, r))
+        if i:
+            landed("ar1%d" % r, V("rq%d" % r, a, b))
 
-    def unpack(r, i):
-        a, b = PARTS[i]
-        for t in range(4):
-            mul(4 * i + t, "eq", "ep", 128 * t, "rq%d" % r, "rs%d" % r, a, b)
+    def unpack(r, i, t):
+        mul(4 * i + t, "eq", "ep", 128 * t, "rq%d" % r, "rs%d" % r, 128 * i, 128 * i + 128)
 
-    def home(r, i):
-        a, b = PARTS[i]
-        for t in range(4):
-            ttt(V("xp", 4 * a + t, 4 * b, 4), by(V("hp", HP * t + CROSS, HP * t + HP), V("own", a // 16, b // 16)), V("xt%d" % r, 4 * a + t, 4 * b, 4), A.add)
+    def meet(r, i, t, q):
+        pick(q, V("xv", C * t + 128 * i, C * t + 128 * i + 128), by(V("xt%d" % r), V("i4", 32 * t + 8 * i, 32 * t + 8 * i + 8)))
 
-    def advance(r, i, some):
+    def home(r, t):
+        ttt(V("xv", C * t + CROSS, C * t + C), by(V("xt%d" % r), V("i4", 32 * t + 16, 32 * t + 20)), V("hw", 64 * t, 64 * t + 64), A.add)
+
+    def join(i, t):
+        v = V("xv", C * t + 128 * i, C * t + 128 * i + 128)
+        ttt(v, bank(4 * i + t, 0, 128), v, A.add)
+
+    def advance(r, i, t, q):
         a, b = PARTS[i]
-        for t in some:
-            ttt(V("xt%d" % (r + 1), 4 * a + t, 4 * b, 4), bank(4 * i + t, 0, b - a), V("xp", 4 * a + t, 4 * b, 4), A.add)
+        pick(q, V("xt%d" % (r + 1), 4 * a + t, 4 * b, 4), by(V("xv", C * t, C * t + C), V("kof%d" % (r + 1), a // 16, b // 16)))
 
     for r in range(ROUNDS):
         register(r)
         n, kof = r + 1, "kof%d" % (r + 1)
-        nm = "nm%d" % r
-        for h in range(2):
-            tts(V(nm, 10 * h, 10 * h + 10), V("sc", 5 - h, 60, 6), 160.0, A.add, float(CROSS), A.min)
-        send(peer[r], V("rn%d" % r), V(nm), "arn%d" % r)
-        landed("arn%d" % r, V("rn%d" % r))
         for h in range(2):
             tts(V("tof", 10 * h, 10 * h + 10), V("sc", 2 + h, 60, 6), 160.0, A.add)
         for h in range(2):
             tts(V(kof, 10 * h, 10 * h + 10), V("sc", 5 - h, 60, 6), 160.0, A.add)
-        if n < ROUNDS:
-            share(n)
-        if r == 0:
-            pairs(0, CROSS, range(4))
-        else:
-            for t in range(4):
-                act(V("zt", 512 + t, 1024, 4), by(V("zc", C * t, C * t + C), V("tof", 8, 16)))
-            pairs(0, 128, range(4))
+        for i in range(2):
+            for t in (2, 3):
+                o = ZW * (t - 2) + CROSS * i
+                act(V("zt", 512 * i + t, 512 * i + 512, 4), by(V("zc", o, o + (C if i else CROSS)), V("tof", 8 * i, 8 * i + 8)))
+        pairs(0, 128, [0, 1])
+        pairs(128, CROSS, [0])
+        quant("zq", "zs", 0, 128, "zt", 0)
+        layer(0, 128, 4, range(4))
+        pairs(128, CROSS, [1])
         pairs(CROSS, C, [0])
-        quant("zq", "zs", 0, CROSS, "zt", 0)
-        layer(0, CROSS, 0, [0, 2, 1, 3])
-        pairs(CROSS, C, [1, 2, 3])
-        for t, q in ((0, "a"), (2, "v"), (1, "a"), (3, "v")):
-            keep(q, V("hp", HP * t, HP * t + CROSS), bank(t, 0, CROSS))
-            if t == 2:
-                quant("zq", "zs", 256, 384, "zt", 192)
-                layer(256, 128, 4, range(4))
-        tts(V("own"), V(kof), float(16 - CROSS), A.add)
-        for t, q in ((0, "a"), (2, "v"), (1, "a"), (3, "v")):
-            lay(r, 0, t, q)
-        lay(r, 1, 0, "a")
-        lay(r, 1, 1, "a")
-        ship(r, 0)
-        lay(r, 1, 2, "v")
-        lay(r, 1, 3, "v")
-        lists = scores_list(kof) + fours(kof) if n < ROUNDS else []
-        run(lists[:2])
-        ship(r, 1)
-        for t in range(4):
-            keep("a", V("hp", HP * t + CROSS + 16, HP * t + HP), bank(4 + t, 64, 128))
-        if n < ROUNDS:
-            run(lists[2:] + partner_list(n))
-        else:
-            act(V("kpf"), by(V("yrow"), V(kof)))
-            dma("s", "okp", [(T.kp[:, :], (T.kpf[0:128:16, :], V("kpf")[1]))])
-            quant("vq", "vs", 0, 128, "vb", 0)
+        quant("zq", "zs", 128, CROSS, "zt", 128)
+        layer(128, 128, 0, range(4))
+        NV = V("nv", 16, 16 + C)
+        if r:
+            act(V("kr", 0, C, 2), by(V("t1"), V("tof", 0, 10)))
+
+        def scatter(h):
+            k, c = V(kof, 10 * h, 10 * h + 10), V("ym", HALF * h, HALF * h + HALF)
+            op("v", lambda e: e.tensor_copy(NV[0].indirect(k[0]), c[0]), NV, k, c)
         if r == 0:
-            quant("eq", "ep", 0, 512, "eb", 0)
-        home(r, 0)
-        unpack(r, 0)
-        home(r, 1)
-        unpack(r, 1)
-        advance(r, 0, range(4))
+            scatter(0)
+        for t in range(4):
+            keep("v" if r and t != 1 else "a", V("ht", t, 512, 4), bank(4 + t, 0, 128))
+        if r:
+            act(V("kr", 1, C, 2), by(V("t1"), V("tof", 10, 20)))
+        pairs(CROSS, C, [1])
+        for t, q in ((0, "a"), (2, "v"), (1, "a"), (3, "v")):
+            if t == 2:
+                ship(r, 0)
+            keep(q if r else "a", V("ht", 512 + t, 1024, 4), bank(t, 0, 128))
+        if r:
+            act(NV, by(V("kr"), V("ki2", 0, 20)))
+            pairs(CROSS, C, [2])
+        else:
+            scatter(1)
+        ship(r, 1)
+        pairs(CROSS, C, [3] if r else [2, 3])
+        run(flips("ta", 0, "nv", 16, 128) + flips("ta", CH, "nv", 16 + 128, 192))
+        if n == ROUNDS:
+            act(V("kpf"), by(V("yrow"), V(kof, 0, 20)))
+            dma("s", "okp", [(T.kp[:, :], (T.kpf[0:128:16, :], V("kpf")[1]))])
+        quant("zq", "zs", 256, 384, "zt", 192)
+        layer(256, 128, 4, range(4))
+        for t in (2, 3, 0, 1):
+            tts(V("i4", 32 * t, 32 * t + 32), by(V("ta"), V("sel", 10, 12)), 4.0, A.mult, 640.0 + t, A.add)
         if n < ROUNDS:
+            tts(V(kof, 20, 52), by(V("ta"), V("sel", 10, 12)), 160.0, A.add)
+            share(n)
+        for i, t, q in ((0, 2, "a"), (0, 0, "v"), (0, 3, "a"), (0, 1, "a"), (1, 2, "a"), (1, 3, "a"), (1, 0, "a"), (1, 1, "a")):
+            meet(r, i, t, q)
+        for t in (2, 3, 0, 1):
+            keep("v", V("hw", 64 * t, 64 * t + 64), bank(4 + t, 64, 128))
+        for t in (2, 3, 0, 1):
+            home(r, t)
+        for i, t in ((0, 2), (0, 3), (0, 0), (1, 2), (1, 3), (1, 0), (0, 1), (1, 1)):
+            unpack(r, i, t)
+            join(i, t)
+        for i, t, q in ((0, 2, "a"), (0, 3, "a"), (0, 0, "v"), (0, 1, "v"), (1, 2, "a"), (1, 0, "v"), (1, 3, "a"), (1, 1, "a")):
+            advance(r, i, t, q)
+        if n < ROUNDS:
+            lists = scores_list(kof) + fours(kof)
             scores(n, 0)
-            advance(r, 1, range(4))
+            run(lists[:2])
             scores(n, 1)
+            run(lists[2:4])
+            signs(lists[4:])
         else:
             for i in range(2):
                 a, b = PARTS[i]
-                if i == 1:
-                    advance(r, 1, range(4))
                 quant("xq", "xs", a, b, "xt%d" % n, a)
                 mul(i, "vq", "vs", 0, "xq", "xs", a, b)
-                act(V("yo", a, b), bank(i, 0, b - a))
                 dma("s", "oc%d" % i, [(T.oc[:, 4 * a:4 * b], raw(V("xq", a, b)))])
+                if i == 0:
+                    act(V("yo", a, b), bank(i, 0, b - a))
+                else:
+                    for j in range(4):
+                        dma("sa"[j % 2], "os", [(T.osc[4 * j:4 * j + 4, :], (T.xs[32 * j:32 * j + 4, :], V("xs")[1]))])
+                    tts(V("yo", a, b), bank(i, 0, b - a), 0.0, A.add)
                 dma("a", "oy%d" % i, [(T.y[:, a:b], V("yo", a, b))])
-            dma("s", "os", [(T.osc[4 * i:4 * i + 4, :], (T.xs[32 * i:32 * i + 4, :], V("xs")[1])) for i in range(4)])
     for sem in total:
         if seen["g"].get(sem, 0) < total[sem]:
             g.wait_ge(T.sem[sem], total[sem])

from concourse.mybir import dt, AluOpType, ActivationFunctionType

C, HALF, CROSS = 320, 160, 256
ROUNDS = 3
MASKS = [1, 2, 3]
LEVELS = [[(4, 1, 2), (14, 1, 2)], [(2, 5, 4)], [(3, 10, 2)], [(1, 15, 2)], [(18, 1, 1)]]
STOPS = [(0, 6, 2), (8, 1, 4), (19, 1, 1)]
RUNS = LEVELS[1] + LEVELS[2] + LEVELS[3] + LEVELS[4] + STOPS + LEVELS[0]
ORDER = [b + s * i for b, s, n in RUNS for i in range(n)]
AT = {b: i for i, b in enumerate(ORDER)}
NL, NF, N1 = 144, 112, 64
RADIX = [4, 3, 3, 3]
BIG, MID, TINY = 1024.0, 168, 2.0 ** -93
T0 = 16 + NL + NF
FAR, CH = 192, 416
G, F0 = 352, 16 + NL
PARTS = [(0, 192), (192, C)]
ZW = CROSS + C
F32, BF, I32, U16, F8, U8 = "float32", "bfloat16", "int32", "uint16", "float8_e4m3fn_x4", "uint8"


def table_at(i):
    return i + 11 if i < 9 else i - 5 if i < 16 else i - 16


def _sb(n, kind):
    return ("sbuf", [128, n], kind)


SCRATCH = {
    "ub": _sb(512, BF), "vb": _sb(512, BF), "uq": _sb(128, F8), "us": _sb(128, U8), "vq": _sb(128, F8), "vs": _sb(128, U8),
    "wq": _sb(512, F8), "wp": _sb(512, U8), "one": _sb(516, BF), "eb": _sb(516, BF), "eq": _sb(512, F8), "ep": _sb(512, U8),
    "pidx": _sb(1, I32), "qidx": _sb(1, I32), "grp": _sb(1, I32), "par": _sb(1, I32), "q8": _sb(1, I32),
    "yrow": _sb(C, F32), "ym": _sb(C, BF), "cst": _sb(16, F32), "sel": _sb(12, U16), "rowc": _sb(112, BF), "lst": _sb(16, F32),
    "ki": _sb(2, I32), "kj": _sb(2, I32), "kf": _sb(2, F32), "tab": _sb(32, F32), "tbm": _sb(40, F32), "pu": _sb(20, U16), "p8": _sb(20, U16),
    "p4": _sb(C, F32), "sb": _sb(C, F32), "bs0": _sb(NL + NF, BF), "bs1": _sb(NF, BF), "bs2": _sb(NF, BF),
    "cw": _sb(16, F32), "ca": _sb(16, F32), "cb": _sb(16, F32), "cd": _sb(16, F32), "ce": _sb(16, F32),
    "c2": _sb(16, F32), "ct0": _sb(16, F32), "ct1": _sb(16, F32),
    "dl": _sb(96, F32), "dat": _sb(96, F32), "sc": _sb(64, F32), "fi": _sb(16, I32), "fa": _sb(16, I32),
    "eo": _sb(32, F32), "ed": _sb(16, F32), "kli": _sb(20, I32), "kw": _sb(32, F32), "kpi": _sb(32, U16), "k4": _sb(128, U16),
    "w0": _sb(T0 + 336, BF), "gg": _sb(2 * G, BF), "bits": _sb(2 * C, BF), "ta": _sb(2 * CH, BF), "tb": _sb(CH, BF),
    "ofa": _sb(16, U16), "ofb": _sb(16, U16), "ofc": _sb(2, U16), "ofl": _sb(16, U16), "ofn": _sb(16, U16), "of0": _sb(16, U16), "of1": _sb(16, U16),
    "kr": _sb(C, BF), "kk": _sb(C, BF), "kd": _sb(400, BF), "tof": _sb(20, U16),
    "yp": _sb(4 * C, BF), "yi": _sb(4 * C, BF), "zc": _sb(2 * ZW, BF), "zt": _sb(4 * C, BF), "zq": _sb(384, F8), "zs": _sb(384, U8),
    "hw": _sb(4 * (C - CROSS), BF), "ht": _sb(4 * CROSS, BF), "xv": _sb(4 * C, BF),
    "nv": _sb(G, BF), "nw": _sb(G, BF), "ki2": _sb(32, U16), "t1": _sb(C, BF), "i4": _sb(128, U16),
    "xq": _sb(C, F8), "xs": _sb(C, U8), "kpf": _sb(C, F32), "yo": _sb(C, F32),
    "ps": ("psum", [128, 4096], F32),
}
for _r in range(ROUNDS + 1):
    SCRATCH["xt%d" % _r] = _sb(4 * C, BF)
    SCRATCH["kof%d" % _r] = _sb(52, U16)
for _r in range(ROUNDS):
    for _n, _k, _w in (("hq", F8, CROSS), ("hs", U8, CROSS), ("rq", F8, CROSS), ("rs", U8, CROSS), ("rk", U16, 40)):
        SCRATCH["%s%d" % (_n, _r)] = _sb(_w, _k)
SEMAPHORES = ["sv", "sa", "sp", "sg", "sent", "lx0", "lx1", "lu", "lv", "lk", "lwc", "lws",
              "oc0", "oc1", "os", "oy0", "oy1", "okp"]
for _r in range(ROUNDS):
    SEMAPHORES += ["ark%d" % _r, "ar0%d" % _r, "ar1%d" % _r]


def rank_program(g, core, T, topo):
    rank = T.rank_of(core)
    if rank is None:
        return
    A, ACT = AluOpType, ActivationFunctionType
    queue = {"v": g.vector, "a": g.scalar, "p": g.tensor, "g": g, "s": g.sync}
    mine = {"v": "sv", "a": "sa", "p": "sp", "g": "sg"}
    total, seen, hist = {}, {q: {} for q in queue}, {}

    def V(nm, a=0, b=None, step=1):
        b = SCRATCH[nm][1][1] if b is None else b
        cols = range(512 * (a // 512), 512 * (a // 512) + 512) if nm == "ps" else range(a, b, step)
        return (T[nm][:, a:b:step] if step > 1 else T[nm][:, a:b], [(nm, sum(1 << c for c in cols))])

    def by(win, off):
        return (win[0].indirect(off[0]), win[1] + off[1])

    def raw(v):
        return (v[0].bitcast(dt.uint8), v[1])

    def ap(x):
        return x[0] if isinstance(x, tuple) else x

    def feet(xs):
        return [f for x in xs if isinstance(x, tuple) for f in x[1]]

    def need(q, reads, writes):
        deps = {}
        for names, isw in ((reads, False), (writes, True)):
            for b, m in names:
                for (em, w, eq, sem, val) in hist.get(b, []):
                    if em & m and (w or isw or (b == "ps" and eq != q)):
                        deps[sem] = max(deps.get(sem, 0), val)
        for sem in deps:
            if seen[q].get(sem, 0) < deps[sem]:
                queue[q].wait_ge(T.sem[sem], deps[sem])
                seen[q][sem] = deps[sem]

    def note(q, reads, writes, sem, val):
        for b, m in writes:
            hist[b] = [e for e in hist.get(b, []) if e[0] & ~m] + [(m, True, q, sem, val)]
        for b, m in reads:
            hist[b] = [e for e in hist.get(b, []) if e[1] or e[3] != sem or e[0] & ~m] + [(m, False, q, sem, val)]

    def op(q, call, out, *ins):
        reads, writes = feet(ins), out[1]
        need(q, reads, writes)
        total[mine[q]] = total.get(mine[q], 0) + 1
        call(queue[q]).then_inc(T.sem[mine[q]], 1)
        note(q, reads, writes, mine[q], total[mine[q]])

    def dma(q, sem, pairs):
        for out, in_ in pairs:
            need(q, feet([in_]), feet([out]))
        for out, in_ in pairs:
            total[sem] = total.get(sem, 0) + 16
            queue[q].dma_start(ap(out), ap(in_)).then_inc(T.sem[sem], 16)
        for out, in_ in pairs:
            note("d" + q, feet([in_]), feet([out]), sem, total[sem])

    def send(dst, out, in_, sem):
        need("g", in_[1], [])
        rid, pid = topo.addr(dst)[0], topo.addr(dst)[1]
        n = len(topo.engines(core, dst))
        g.remote_dma(out[0], in_[0], T.sem[sem], T.sem.sent, pid, rid, topo.mask(core, dst))
        total["sent"] = total.get("sent", 0) + n
        total[sem] = total.get(sem, 0) + n

    def landed(sem, *views):
        note("net", [], feet(views), sem, total[sem])

    def tts(out, in0, s1, o0, s2=None, o1=None):
        tail = (o0,) if o1 is None else (o0, o1)
        op("v", lambda e: e.tensor_scalar(out[0], in0[0], ap(s1), ap(s2), *tail), out, in0, s1, s2)

    def ttt(out, in0, in1, o):
        op("v", lambda e: e.tensor_tensor(out[0], in0[0], in1[0], o), out, in0, in1)

    def fill(out, x):
        op("v", lambda e: e.memset(out[0], x), out)

    def act(out, in_, f=ACT.Copy, **k):
        op("a", lambda e: e.activation(out[0], in_[0], f, **{n: ap(k[n]) for n in k}), out, in_, *k.values())

    def iota(out, pattern, base, mult, **k):
        op("g", lambda e: e.iota(out[0], pattern, base, mult, **k), out)

    def quant(q, s, a, b, t, ta, shift=0):
        qv, sv, tv = V(q, a, b), V(s, a, b), V(t, 4 * ta + shift, 4 * (ta + b - a) + shift)
        op("v", lambda e: e.quantize_mx(qv[0], sv[0], tv[0]), (None, qv[1] + sv[1]), tv)

    def bank(i, a, b):
        return V("ps", 512 * i + a, 512 * i + b)

    def mul(i, lq, ls, l, rq, rs, a, b):
        x = [V(lq, l, l + 128), V(ls, l, l + 128), V(rq, a, b), V(rs, a, b)]
        out = bank(i, 0, b - a)
        op("p", lambda e: e.matmul_mx(out[0], x[0][0], x[1][0], x[2][0], x[3][0], True, True), out, *x)

    def flip(out, in_):
        op("v", lambda e: e.transpose(out[0], in_[0]), out, in_)

    def flips(to, at, nm, c, n):
        n1, n2 = 32 * ((n + 31) // 32), 32 * ((n + 47) // 32)
        return [lambda: flip(V(to, at, at + n1), V(nm, c, c + n1)), lambda: flip(V(to, at + FAR, at + FAR + n2), V(nm, c - 16, c - 16 + n2))]

    def wrapped(out, to, at, mult, plus, chunks=1):
        tts(out, by(V(to, at, at + chunks * CH), V("sel", 0, chunks)), mult, A.mult, plus, A.add)

    def run(calls):
        for call in calls:
            call()

    later = []

    def drip(n=1):
        now = later[:n]
        later[:n] = []
        run(now)

    def col(i):
        return V("cst", i, i + 1)

    peer = [T.cores[rank ^ m] for m in MASKS]
    dma("s", "lx0", [(V("xt0", 0, 768), T.x[:, 0:768])])
    dma("a", "lk", [(V("kli"), T.kl[:, :])])
    dma("a", "lu", [(V("ub"), T.u[:, :])])
    dma("s", "lx1", [(V("xt0", 768, 1280), T.x[:, 768:1280])])
    need("s", V("xt0")[1] + V("ub")[1], [])
    dma("s", "lwc", [(raw(V("wq")), T.wc[:, 0:2048])])
    dma("s", "lws", [(V("wp"), T.ws[:, 0:512])])
    dma("s", "lv", [(V("vb"), T.v[:, :])])

    small = {"allow_small_or_imprecise_dtypes": True}
    Q, GR = V("qidx"), V("grp")
    iota(V("pidx"), [[0, 1]], 0, 1)
    iota(V("yrow"), [[1, C]], 0, 0, **small)
    for b, s, n in RUNS:
        iota(V("tab", b, b + s * (n - 1) + 1, s), [[32 * (1 - s), n]], 32 * (table_at(AT[b]) - b) - 2 * MID, 0, **small)
    fill(V("one"), 1.0)
    fill(V("rowc"), 0.0)
    fill(V("kw"), 0.0)
    tts(Q, V("pidx"), 15, A.bitwise_and)
    tts(GR, V("pidx"), 4, A.arith_shift_right)
    tts(V("q8"), V("pidx"), 3, A.arith_shift_right, 1, A.bitwise_and)
    tts(col(0), Q, 0.0, A.is_equal)
    tts(col(5), GR, 1.0, A.mult)
    tts(col(9), Q, 1.0, A.mult)
    tts(col(10), Q, 11.0, A.min, 16.0, A.mult)
    tts(col(11), V("q8"), 1.0, A.mult)
    tts(col(7), col(0), 3.0, A.mult, 1.0, A.add)
    tts(V("par"), Q, col(5), A.add)

    def blank(nm, a, b):
        for c in range(a, b, 512):
            act(V(nm, c, min(b, c + 512)), V("one", 0, min(b - c, 512)), scale=0.0)
    blank("tb", 0, CH)
    for i, (b, s, n) in enumerate(RUNS):
        out = V("rowc", 64 + AT[b], 64 + AT[b] + n)
        if i < 4:
            act(out, V("yrow", b, b + s * (n - 1) + 1, s))
        else:
            tts(out, V("yrow", 0, n), float(s), A.mult, float(b), A.add)
    tts(V("par"), V("par"), 1, A.bitwise_and)
    tts(col(8), col(0), 32.0 * (20 - table_at(AT[0])), A.mult)
    tts(col(2), col(0), 2.0, A.mult)
    tts(col(6), col(0), 2.0 * (N1 - MID) - BIG, A.mult, BIG, A.add)
    tts(V("sel", 0, 1), V("par"), float(FAR + 16), A.mult, col(10), A.add)
    tts(V("pu"), V("rowc", 64, 84), 16.0, A.mult, col(9), A.add)
    tts(V("p8"), V("rowc", 64, 84), 2.0, A.mult, col(11), A.add)
    blank("w0", 0, 16)
    act(V("p4"), by(V("yrow"), V("pu")), ACT.Identity, scale=col(7))
    for b in (0, 10):
        v = V("p4", 16 * AT[b] + 4, 16 * AT[b] + 8)
        act(v, v, ACT.Identity, bias=col(8))
    run(flips("tb", 0, "rowc", 64, 32))
    tts(col(3), col(0), -1.0, A.mult)
    tts(col(4), col(0), TINY, A.mult)
    tts(col(1), col(0), BIG, A.mult)
    wrapped(V("lst"), "tb", 0, 1.0, 0.0)

    def scores_list(k):
        return [lambda: tts(V("kw", 0, 10), V(k, 0, 10), 0.0, A.add), lambda: tts(V("kw", 10, 20), V(k, 0, 10), float(C), A.add),
                lambda: tts(V("kpi"), by(V("kw"), V("sel", 2, 4)), 0.0, A.add)]

    def share(r):
        w = 40 if r else 20
        send(peer[r], V("rk%d" % r, 0, w), V("kof%d" % r, 0, w), "ark%d" % r)
        landed("ark%d" % r, V("rk%d" % r, 0, w))

    for b, s, n in RUNS:
        iota(V("rowc", 16 + b, 16 + b + s * (n - 1) + 1, s), [[1, n]], AT[b] + (CH // 16 - 8) * (AT[b] >= 8), 0, **small)
    blank("gg", F0 + NF, G + F0)
    blank("gg", G + F0 + NF, 2 * G)
    act(V("w0", T0 + N1, T0 + N1 + NF), V("yrow", 0, NF), ACT.Identity, scale=col(2), bias=col(6))
    for a in (128, 352):
        blank("ta", a, a + 64)
    iota(V("dl"), [[0, 16], [-1, 2], [0, 3]], 0, 0, **small)
    LH = V("lst", 0, 4, 2)
    CW = V("cw")
    second = [
        lambda: run(flips("tb", 0, "rowc", 16, 48)),
        lambda: wrapped(V("lst"), "tb", 0, 1.0, 0.0),
        lambda: tts(V("ki"), LH, col(5), A.add),
        lambda: tts(V("kj"), V("ki"), 1, A.bitwise_and),
        lambda: tts(V("kf"), V("kj"), float(FAR // 16 + 1), A.mult),
        lambda: ttt(V("kf"), V("kf"), LH, A.add)]
    rest = [
        lambda: tts(V("sel", 4, 5), V("kf", 0, 1), 16.0, A.mult),
        lambda: tts(V("sel", 6, 10, 2), V("kf"), 16.0, A.mult, 1.0, A.add),
        lambda: tts(V("sel", 1, 2), V("sel", 0, 1), float(CH), A.add),
        lambda: tts(V("c2"), CW, 2.0, A.mult, -160.0, A.add),
        lambda: tts(V("dat", 3, 96, 6), CW, 4.0, A.mult, -319.0, A.add),
        lambda: tts(V("ca"), CW, 0.0, A.is_equal),
        lambda: tts(V("ce"), CW, 159.0, A.is_equal, 2.0, A.mult),
        lambda: tts(V("cb"), CW, 159.0, A.is_equal, -160.0, A.mult),
        lambda: ttt(V("ca"), CW, V("ca"), A.subtract),
        lambda: tts(V("dl", 1, 96, 6), V("ce"), -1.0, A.add),
        lambda: tts(V("cd"), CW, 159.0, A.is_equal, 161.0, A.mult),
        lambda: ttt(V("ct0"), V("ca"), V("cb"), A.add),
        lambda: ttt(V("ct1"), V("ca"), V("cd"), A.add)]
    natural = [
        lambda: (tts(col(14), V("par"), float(FAR + 16), A.mult), tts(col(13), Q, 3.0, A.min, 16.0, A.mult)),
        lambda: (tts(col(12), col(11), float(CH - 128), A.mult, col(14), A.add),
                 tts(V("sel", 11, 12), col(13), col(14), A.add, float(CH + 128), A.add)),
        lambda: tts(V("sel", 10, 11), Q, 16.0, A.mult, col(12), A.add)]

    def scores(r, i, between=list):
        a, b = PARTS[i]
        quant("xq", "xs", a, b, "xt%d" % r, a)
        between()
        for j in range(1 + i):
            mul(i + j, "uq", "us", 0, "xq", "xs", a, b)
        if i:
            act(V("bits", C + a, C + b), bank(i, 0, b - a), ACT.Sign, scale=col(3), bias=col(4))

    def signs(between):
        (a, b), (c, d) = PARTS
        tts(V("bits", a, b), bank(0, 0, b - a), 0.0, A.is_gt, col(2), A.mult)
        run(between)
        tts(V("bits", C + a, C + b), V("bits", a, b), -1.0, A.mult, col(0), A.add)
        tts(V("bits", c, d), bank(2, 0, d - c), 0.0, A.is_gt, col(2), A.mult)

    def fours(k):
        return [lambda t=t: tts(V("k4", 32 * t, 32 * t + 20), V(k, 0, 20), 4.0, A.mult, float(t), A.add) for t in range(4)]

    calls = scores_list("kli")
    tts(V("kof0", 0, 20), V("kli"), 0.0, A.add)
    run(calls[:2])
    tts(V("sel", 2, 4), V("lst", 0, 2), 0.0, A.add)
    tts(V("tbm", 0, 20), V("tab", 0, 20), col(0), A.mult)
    tts(V("tbm", 20, 40), V("tab", 0, 20), float(1 - 2 * C), A.add, col(0), A.mult)
    tts(CW, V("yrow", 0, 16), 16.0, A.mult, col(9), A.add)
    run(calls[2:])
    scores(0, 0, lambda: quant("uq", "us", 0, 128, "ub", 0))
    for a in (0, HALF):
        ttt(V("sb", a, a + HALF), by(V("tbm"), V("p8", a // 16, a // 16 + 10)), V("p4", a, a + HALF), A.add)
        if a == 0:
            scores(0, 1)
    signs(fours("kli")[1:])
    act(V("rowc", 48, 64), V("rowc", 26, 42))
    act(V("bs0"), V("sb", 0, NL + NF), ACT.Identity, bias=col(1))
    run(fours("kli")[:1])
    share(0)
    op("g", lambda e: e.affine_select(T.eb[:], T.one[:], [[1, 516]], A.is_equal, 0.0, -3, -4), V("eb"), V("one"))
    for t in range(2):
        iota(V("zc", ZW * t + CROSS + 192, ZW * t + 2 * CROSS), [[0, 64]], 0, 0, **small)
    iota(V("nv"), [[0, G]], 0, 0, **small)
    for a in (0, G - 16):
        iota(V("nw", a, a + 16), [[0, 16]], 0, 0, **small)
    iota(V("t1"), [[1, HALF], [HALF, 2]], -HALF, 0, **small)

    def partner_list(r):
        return [lambda: act(V("kr"), by(V("ym"), V("rk%d" % r, 0, 20))), lambda: act(V("kk"), by(V("kr"), V("kof%d" % r, 0, 20)))] + [
            lambda h=h: act(V("kd", 16 + 192 * h, 16 + 192 * h + HALF), V("kk", h, C, 2)) for h in range(2)]

    def register(r):
        xt = "xt%d" % r

        def half(t):
            act(V("yp", C * t, C * t + C), by(V(xt), V("k4", 32 * t, 32 * t + 20)), scale=0.5)

        def again(t, a):
            act(V("yi", C * t + a, C * t + C), V("yp", C * t + a, C * t + C))

        def level(at, n, off):
            to = T0 + N1 + NF + at
            ttt(V("w0", to, to + n), by(V("w0", T0, to), off), V("bs0", at, at + n), A.min)

        def both(t, a, at, lo, hi, c):
            o, z = C * t, ZW * (t - 2) + at
            ttt(V("zc", z + lo + a, z + hi, 2), V("yp", o + lo + a, o + hi, 2), V("yp", o + c, o + c + (hi - lo) // 2), A.add)

        def beside(calls, small):
            return [lambda c=c, s=small[i:i + 1]: (c(), run(s)) for i, c in enumerate(calls)]

        def group(calls, n):
            return [lambda c=c: run(calls[c:c + n]) for c in range(0, len(calls), n)]
        for a, b in ((0, HALF), (HALF, C)):
            ttt(V("w0", 16 + a, 16 + b), by(V("bits"), V("kpi", a // 16, b // 16)), V("sb", a, b), A.add)
        for t in (2, 3, 0, 1):
            half(t)
        sums = [lambda t=t, a=a, w=w: both(t, a, *w) for t in (2, 3) for w in ((CROSS, 0, 192, HALF), (0, 0, CROSS, 0)) for a in range(2)]
        few = [lambda t=t, a=a: both(t, a, CROSS, CROSS, C, 128) for t in (2, 3) for a in range(2)] + [list] * 4

        def flags():
            op("v", lambda e: e.tensor_copy(T.fi[:], T.ta[:, 0:2 * CH].indirect(T.sel[:, 4:5])), V("fi"), V("ta"), V("sel", 4, 5))
        later.extend(beside(second, [list, rest[5]] + group(rest[6:8], 2) + group([rest[8], rest[3], rest[9], rest[4]], 2) + natural[:1]) if r == 0 else [list, list] + sums[:2] + [lambda: (flags(), run(few[:2]))])
        run(flips("ta", 0, "w0", 16, 128))
        more = flips("ta", CH, "w0", 16 + 128, 192)
        more[0]()
        drip()
        wrapped(V("ofa"), "ta", 0, 0.5, float(MID))
        more[1]()
        drip()
        level(0, 64, V("ofa", 0, 4))
        wrapped(V("ofb"), "ta", CH, 0.5, float(MID))
        wrapped(V("ofl"), "ta", CH, 0.5, float(MID - N1))
        level(64, 32, V("ofa", 4, 6))
        tts(V("ofc"), V("ofb", 0, 2), float(N1 + NF + 127), A.min)
        drip()
        level(96, 32, V("ofa", 6, 8))
        drip()
        level(128, 32, V("ofc"))
        drip()
        ttt(V("gg", F0 - 16, F0 + NF), by(V("w0", T0, T0 + 336), V("ofb", 0, 8)), V("bs0", 128, 256), A.min)
        signed = [
            flags, lambda: run(flips("ta", 0, "w0", T0 + N1 + NF, NL)),
            lambda: (tts(V("fa"), V("fi"), 1, A.arith_shift_right, 1, A.bitwise_and), wrapped(V("ofn"), "ta", 0, 0.5, float(MID - N1))),
            lambda: (ttt(V("dat", 2, 96, 6), V("fa"), V("c2"), A.add), tts(V("dl", 2, 96, 6), V("fa"), -2.0, A.mult, 1.0, A.add))]
        tail = [
            lambda: run(flips("ta", 0, "kd", 16, HALF)), lambda: run(flips("ta", CH, "kd", 16 + 192, HALF)),
            lambda: wrapped(V("eo"), "ta", 0, 1.0, 0.0, 2),
            lambda: (ttt(V("dl", 4, 96, 6), V("eo", 16, 32), V("eo", 0, 16), A.subtract),
                     ttt(V("dat", 5, 96, 6), V("eo", 16, 32), V("eo", 0, 16), A.add)),
            lambda: ttt(V("ed"), V("dl", 4, 96, 6), V("c2"), A.mult),
            lambda: ttt(V("dat", 4, 96, 6), V("eo", 0, 16), V("ed"), A.subtract)]
        pl = partner_list(r)
        aside = [lambda: run(pl[:2]), lambda: (run(pl[2:]), again(0, 0)), lambda: (again(1, 0), again(2, CROSS)), lambda: again(3, CROSS)]
        if r == 0:
            act(V("ym"), V("yrow"), ACT.Identity, bias=-160.0)
            aside = [lambda: (again(0, 0), again(1, 0), blank("kd", 0, 400)), aside[0], lambda: (run(pl[2:]), again(2, CROSS)), aside[3]]
            small = group(rest[:3], 3) + beside(signed, group([rest[10], few[0]], 2) + rest[11:] + few[1:]) + tail[:2] + beside(tail[2:4], few[2:])
            sums[:2] = beside(sums[:2], natural[1:])
            for i in range(5):
                later.extend(small[i:i + 1] + sums[i:i + 1])
            later.extend(sums[5:6] + small[5:7] + sums[6:7] + small[7:8] + sums[7:] + small[8:])
        else:
            aside[2] = lambda: (act(V("nw", 16, 16 + C), by(V("nv", 16, 16 + C), V("rk%d" % r, 20, 40))), again(1, 0))
            aside[3] = lambda: (again(2, CROSS), again(3, CROSS))
            through = [lambda: run(flips("ta", 0, "nw", 16, 128)), lambda: run(flips("ta", CH, "nw", 16 + 128, 192)),
                       lambda: tts(V("ki2"), by(V("ta"), V("sel", 10, 12)), 160.0, A.add)]
            later.extend(sums[2:3] + signed[1:3] + sums[3:4] + beside(signed[3:], few[2:]) + sums[4:6] + few[3:4] + sums[6:7]
                         + tail[:2] + sums[7:] + tail[2:4] + through + tail[4:] + [list])
            later.append((lambda: quant("vq", "vs", 0, 128, "vb", 0)) if r == 1 else list)
        cur, nxt = F0, G + F0
        for i, rad in enumerate(RADIX):
            base, of = V("bs%d" % (1 + i % 2)), "of%d" % (i % 2)
            drip()
            act(base, V("gg", cur, cur + NF), ACT.Identity, bias=col(1))
            aside[i]()
            run(flips("tb", 0, "gg", cur, NF))
            drip()
            wrapped(V(of), "tb", 0, 0.5, float(MID - N1))
            for j in range(rad - 1):
                drip()
                ttt(V("gg", nxt, nxt + NF), by(V("gg", cur, cur + NF), V(of, 0, NF // 16)), base, A.min)
                cur, nxt = nxt, cur
        if r == 0:
            later.extend(beside(tail[4:] + [list, list], [lambda b=b: quant("eq", "ep", 128 * b, 128 * b + 128, "eb", 0, 3 - b) for b in range(4)]))
        drip(max(len(later) - 4, 1))
        low = V("gg", cur, cur + NF)
        act(V("gg", cur + NF, cur + NF + N1), by(low, V("ofl", 8, 12)))
        tts(V("gg", cur - NL, cur), by(low, V("ofn", 0, NL // 16)), 0.0, A.add)
        drip()
        run(flips("ta", 0, "gg", cur - NL, 128) + flips("ta", CH, "gg", cur - 16, 192))
        drip()
        for c, ct, sl in ((8, "ct1", 0), (6, "ct0", 1)):
            ttt(V("dat", sl, 96, 6), by(V("ta"), V("sel", c, c + 1)), V(ct), A.is_equal)
        drip()
        op("v", lambda e: e.tensor_tensor_scan(T.sc[:, 0:60], T.dl[:, 0:60], T.dat[:, 0:60], 0.0, A.mult, A.add),
           V("sc", 0, 60), V("dl", 0, 60), V("dat", 0, 60))
        drip(len(later))

    def pairs(a, b, some):
        for t in some:
            ttt(V("zt", 4 * a + t, 4 * b, 4), by(V("yp", C * t, C * t + C), V("tof", a // 16, b // 16)), V("yi", C * t + a, C * t + b), A.add)

    def layer(zcol, n, bk, some):
        for b in some:
            mul(bk + b, "wq", "wp", 128 * b, "zq", "zs", zcol, zcol + n)

    def keep(q, out, src):
        if q == "a":
            act(out, src, scale=0.03125)
        else:
            tts(out, src, 0.03125, A.mult)

    def pick(q, out, src):
        if q == "a":
            act(out, src)
        else:
            tts(out, src, 0.0, A.add)

    def ship(r, i):
        a, b = 128 * i, 128 * i + 128
        quant("hq%d" % r, "hs%d" % r, a, b, "ht", a)
        if i:
            send(peer[r], V("rs%d" % r), V("hs%d" % r), "ar0%d" % r)
            landed("ar0%d" % r, V("rq%d" % r, 0, 128), V("rs%d" % r))
        send(peer[r], raw(V("rq%d" % r, a, b)), raw(V("hq%d" % r, a, b)), "ar%d%d" % (i, r))
        if i:
            landed("ar1%d" % r, V("rq%d" % r, a, b))

    def unpack(r, i, t):
        mul(4 * i + t, "eq", "ep", 128 * t, "rq%d" % r, "rs%d" % r, 128 * i, 128 * i + 128)

    def meet(r, i, t, q):
        pick(q, V("xv", C * t + 128 * i, C * t + 128 * i + 128), by(V("xt%d" % r), V("i4", 32 * t + 8 * i, 32 * t + 8 * i + 8)))

    def home(r, t):
        ttt(V("xv", C * t + CROSS, C * t + C), by(V("xt%d" % r), V("i4", 32 * t + 16, 32 * t + 20)), V("hw", 64 * t, 64 * t + 64), A.add)

    def join(i, t):
        v = V("xv", C * t + 128 * i, C * t + 128 * i + 128)
        ttt(v, bank(4 * i + t, 0, 128), v, A.add)

    def advance(r, i, t, q):
        a, b = PARTS[i]
        pick(q, V("xt%d" % (r + 1), 4 * a + t, 4 * b, 4), by(V("xv", C * t, C * t + C), V("kof%d" % (r + 1), a // 16, b // 16)))

    for r in range(ROUNDS):
        register(r)
        n, kof = r + 1, "kof%d" % (r + 1)
        for h in range(2):
            tts(V("tof", 10 * h, 10 * h + 10), V("sc", 2 + h, 60, 6), 160.0, A.add)
        for h in range(2):
            tts(V(kof, 10 * h, 10 * h + 10), V("sc", 5 - h, 60, 6), 160.0, A.add)
        for i in range(2):
            for t in (2, 3):
                o = ZW * (t - 2) + CROSS * i
                act(V("zt", 512 * i + t, 512 * i + 512, 4), by(V("zc", o, o + (C if i else CROSS)), V("tof", 8 * i, 8 * i + 8)))
        pairs(0, 128, [0, 1])
        pairs(128, CROSS, [0])
        quant("zq", "zs", 0, 128, "zt", 0)
        layer(0, 128, 4, range(4))
        pairs(128, CROSS, [1])
        pairs(CROSS, C, [0])
        quant("zq", "zs", 128, CROSS, "zt", 128)
        layer(128, 128, 0, range(4))
        NV = V("nv", 16, 16 + C)
        if r:
            act(V("kr", 0, C, 2), by(V("t1"), V("tof", 0, 10)))

        def scatter(h):
            k, c = V(kof, 10 * h, 10 * h + 10), V("ym", HALF * h, HALF * h + HALF)
            op("v", lambda e: e.tensor_copy(NV[0].indirect(k[0]), c[0]), NV, k, c)
        if r == 0:
            scatter(0)
        for t in range(4):
            keep("v" if r and t != 1 else "a", V("ht", t, 512, 4), bank(4 + t, 0, 128))
        if r:
            act(V("kr", 1, C, 2), by(V("t1"), V("tof", 10, 20)))
        pairs(CROSS, C, [1])
        for t, q in ((0, "a"), (2, "v"), (1, "a"), (3, "v")):
            if t == 2:
                ship(r, 0)
            keep(q if r else "a", V("ht", 512 + t, 1024, 4), bank(t, 0, 128))
        if r:
            act(NV, by(V("kr"), V("ki2", 0, 20)))
            pairs(CROSS, C, [2])
        else:
            scatter(1)
        ship(r, 1)
        pairs(CROSS, C, [3] if r else [2, 3])
        run(flips("ta", 0, "nv", 16, 128) + flips("ta", CH, "nv", 16 + 128, 192))
        if n == ROUNDS:
            act(V("kpf"), by(V("yrow"), V(kof, 0, 20)))
            dma("s", "okp", [(T.kp[:, :], (T.kpf[0:128:16, :], V("kpf")[1]))])
        quant("zq", "zs", 256, 384, "zt", 192)
        layer(256, 128, 4, range(4))
        for t in (2, 3, 0, 1):
            tts(V("i4", 32 * t, 32 * t + 32), by(V("ta"), V("sel", 10, 12)), 4.0, A.mult, 640.0 + t, A.add)
        if n < ROUNDS:
            tts(V(kof, 20, 52), by(V("ta"), V("sel", 10, 12)), 160.0, A.add)
            share(n)
        for i, t, q in ((0, 2, "a"), (0, 0, "v"), (0, 3, "a"), (0, 1, "a"), (1, 2, "a"), (1, 3, "a"), (1, 0, "a"), (1, 1, "a")):
            meet(r, i, t, q)
        for t in (2, 3, 0, 1):
            keep("v", V("hw", 64 * t, 64 * t + 64), bank(4 + t, 64, 128))
        for t in (2, 3, 0, 1):
            home(r, t)
        for i, t in ((0, 2), (0, 3), (0, 0), (1, 2), (1, 3), (1, 0), (0, 1), (1, 1)):
            unpack(r, i, t)
            join(i, t)
        for i, t, q in ((0, 2, "a"), (0, 3, "a"), (0, 0, "v"), (0, 1, "v"), (1, 2, "a"), (1, 0, "v"), (1, 3, "a"), (1, 1, "a")):
            advance(r, i, t, q)
        if n < ROUNDS:
            lists = scores_list(kof) + fours(kof)
            scores(n, 0)
            run(lists[:2])
            scores(n, 1)
            run(lists[2:4])
            signs(lists[4:])
        else:
            for i in range(2):
                a, b = PARTS[i]
                quant("xq", "xs", a, b, "xt%d" % n, a)
                mul(i, "vq", "vs", 0, "xq", "xs", a, b)
                dma("s", "oc%d" % i, [(T.oc[:, 4 * a:4 * b], raw(V("xq", a, b)))])
                if i == 0:
                    act(V("yo", a, b), bank(i, 0, b - a))
                else:
                    for j in range(4):
                        dma("sa"[j % 2], "os", [(T.osc[4 * j:4 * j + 4, :], (T.xs[32 * j:32 * j + 4, :], V("xs")[1]))])
                    tts(V("yo", a, b), bank(i, 0, b - a), 0.0, A.add)
                dma("a", "oy%d" % i, [(T.y[:, a:b], V("yo", a, b))])
    for sem in total:
        if seen["g"].get(sem, 0) < total[sem]:
            g.wait_ge(T.sem[sem], total[sem])
